import numpy as np
import ml_dtypes


def mxq(x, axis, fmt="e4m3"):
    dtype, down = {"e4m3": (ml_dtypes.float8_e4m3fn, 7), "e5m2": (ml_dtypes.float8_e5m2, 14)}[fmt]
    v = np.moveaxis(np.asarray(x, np.float32).astype(ml_dtypes.bfloat16).astype(np.float64), axis, -1)
    blocks = v.reshape(v.shape[:-1] + (-1, 32))
    amax = np.abs(blocks).max(-1, keepdims=True)
    byte = np.maximum(np.where(amax > 0, np.frexp(amax)[1] - 1 + 127, 0) - down, 1)
    scale = np.exp2(byte - 127.0)
    codes = (blocks / scale).astype(np.float32).astype(dtype).astype(np.float64)
    return np.moveaxis((codes * scale).reshape(v.shape), -1, axis)


WIDE = False


def mx_kscale(k):
    if not WIDE:
        return np.ones(k)
    levels = np.array([10, -10, 5, -5, 0])
    if k % 512:
        return np.exp2(np.random.permutation(np.resize(levels, k // 32))).repeat(32)
    a = np.empty((k // 512, 16))
    for p in range(k // 512):
        a[p, :8] = np.random.permutation(np.resize(levels, 8))
        for g in range(8):
            far = levels[np.abs(levels - a[p, g]) >= 10]
            a[p, g + 8] = far[np.random.randint(len(far))]
    return np.exp2(a.ravel()).repeat(32)


def f64(x):
    return np.asarray(x).astype(np.float64)


def striped(idx):
    return np.tile(idx.reshape(-1, 16).T, (8, 1)).astype(np.uint16)


def unstriped(offs):
    return offs[:16].T.reshape(-1).astype(np.int64)


E2M1 = np.array([0.0, 0.5, 1.0, 1.5, 2.0, 3.0, 4.0, 6.0, -0.0, -0.5, -1.0, -1.5, -2.0, -3.0, -4.0, -6.0])


def pack_weight(w, fmt):
    k, n = w.shape
    w = f64(np.asarray(w, np.float32).astype(ml_dtypes.bfloat16)).reshape(k // 32, 32, n)
    amax = np.abs(w).max(1)
    if fmt == "e4m3":
        byte = np.frexp(amax)[1] - 1 + 127 - 7
    else:
        mant, ex = np.frexp(amax / 6.0)
        byte = np.where(mant > 0.5, ex, ex - 1) + 127
    byte = np.clip(np.where(amax > 0, byte, 1), 1, 254)
    scaled = (w * np.exp2(127.0 - byte)[:, None, :]).reshape(k, n).astype(np.float32)
    by_word = np.ascontiguousarray(scaled.reshape(k // 512, 128, 4, n).transpose(0, 1, 3, 2))
    if fmt == "e4m3":
        words = by_word.astype(ml_dtypes.float8_e4m3fn).view(np.uint8)
    else:
        c = by_word.astype(ml_dtypes.float4_e2m1fn).view(np.uint8) & 0xF
        words = (c[..., 0::2] | (c[..., 1::2] << 4)).reshape(k // 512, 128, 2 * n)
    return np.ascontiguousarray(words), np.ascontiguousarray(byte.astype(np.uint8).reshape(k // 512, 16, n))


def unpack_weight(words, scales, fmt):
    g, _, n = scales.shape
    words = np.ascontiguousarray(words).reshape(g, 128, n, -1)
    if fmt == "e4m3":
        vals = words.view(ml_dtypes.float8_e4m3fn).astype(np.float64)
    else:
        nib = np.empty((g, 128, n, 4), np.uint8)
        nib[..., 0::2] = words & 0xF
        nib[..., 1::2] = words >> 4
        vals = E2M1[nib]
    vals = vals * np.repeat(np.exp2(scales.astype(np.float64) - 127.0), 8, axis=1)[..., None]
    return vals.transpose(0, 1, 3, 2).reshape(g * 512, n)


K, T, E, N = 1024, 2048, 8, 128
COUNTS = (128, 128, 128, 256, 128, 384, 384, 512)
STARTS = np.cumsum((0,) + COUNTS)
K8 = 512


def by_expert(wq, xq):
    return np.concatenate([wq[e].T @ xq[:, STARTS[e]:STARTS[e + 1]] for e in range(E)], axis=1)


def setup_inputs():
    n = np.random.standard_normal
    s = mx_kscale(K)[:, None]
    expert = np.random.permutation(np.repeat(np.arange(E), COUNTS))
    slot_token = np.argsort(expert, kind="stable")
    w = n((E, K, N)) / np.sqrt(K) / s[None]
    w8 = [pack_weight(m[:K8], "e4m3") for m in w]
    w4 = [pack_weight(m[K8:], "e2m1") for m in w]
    return {
        "xT": (n((K, T)) * s).astype(np.float32),
        "w8_words": np.stack([m[0] for m in w8]),
        "w8_scales": np.stack([m[1] for m in w8]),
        "w4_words": np.stack([m[0] for m in w4]),
        "w4_scales": np.stack([m[1] for m in w4]),
        "b": (0.3 * n((N, E))).astype(np.float32),
        "gate": np.tile(np.random.uniform(0.2, 1.0, T), (N, 1)).astype(np.float32),
        "offs": striped(slot_token),
    }


def reference(xT, w8_words, w8_scales, w4_words, w4_scales, b, gate, offs):
    idx = unstriped(offs)
    w = np.stack([np.concatenate([unpack_weight(w8_words[e], w8_scales[e], "e4m3"), unpack_weight(w4_words[e], w4_scales[e], "e2m1")]) for e in range(E)])
    xq = mxq(f64(xT)[:, idx], 0, "e4m3")
    y = by_expert(w, xq)
    y = y + np.repeat(f64(b), COUNTS, axis=1)
    out = np.zeros((N, T))
    out[:, idx] = f64(gate) * y
    return out

@@ -1,0 +1,162 @@
+from contextlib import ExitStack
+
+import concourse.mybir as mybir
+
+K, T, E, N = 1024, 2048, 8, 128
+COUNTS = (128, 128, 128, 256, 128, 384, 384, 512)
+STARTS = tuple(sum(COUNTS[:e]) for e in range(E + 1))
+FLOPS = 2 * T * K * N
+
+P = 128
+PACK = 4
+BANK = 512
+
+F32 = mybir.dt.float32
+BF16 = mybir.dt.bfloat16
+I32 = mybir.dt.int32
+U32 = mybir.dt.uint32
+U16 = mybir.dt.uint16
+U8 = mybir.dt.uint8
+FP8X4 = mybir.dt.float8_e4m3fn_x4
+FP4X4 = mybir.dt.float4_e2m1fn_x4
+COPY = mybir.ActivationFunctionType.Copy
+IDENTITY = mybir.ActivationFunctionType.Identity
+MULT = mybir.AluOpType.mult
+
+CHUNKS = (
+    ((1024, 576), (512, 224), (512, 272)),
+    ((512, 96), (512, 96), (512, 112), (256, 80), (256, 160)),
+)
+QCOLS = 512
+PIECES = ((0, 1024), (1024, 2048))
+SCATTERS = ((0, 768), (768, 1536), (1536, 2048))
+EARLY = ((0, 768), (768, 1536), (1536, 2048))
+
+
+def tile_moe_rag_lin_bias_kernel(
+    tc, xT, w8_words, w8_scales, w4_words, w4_scales, b, gate, offs, out
+):
+    nc = tc.nc
+    with ExitStack() as ctx:
+        keep = ctx.enter_context(tc.tile_pool(name="keep", bufs=1))
+        psum = ctx.enter_context(tc.psum_pool(name="psum", bufs=1))
+
+        offsets = keep.tile([P, T // 16], U16, name="offsets")
+        w8 = keep.tile([P, E * N * 4], U8, name="w8", align_bytes=64)
+        w4 = keep.tile([P, E * N * 2], U8, name="w4", align_bytes=64)
+        wsc = keep.tile([P, E * N], U8, name="wsc", align_bytes=64)
+        bias = keep.tile([P, E], F32, name="bias")
+        gates = keep.tile([P, T], F32, name="gates")
+        sc = keep.tile([P, T], U8, name="sc", align_bytes=64)
+        gsc = keep.tile([P, T], U8, name="gsc", align_bytes=64)
+        words = [keep.tile([P, T], U32, name=f"words{g}", align_bytes=64) for g in range(2)]
+        gwords = [keep.tile([P, T], U32, name=f"gwords{g}", align_bytes=64) for g in range(2)]
+        xb = [keep.tile([P, T * PACK], BF16, name=f"xb{g}", align_bytes=64) for g in range(2)]
+        y = keep.tile([P, T], F32, name="y")
+        win = keep.tile([P, T], F32, name="win")
+        banks = [psum.tile([P, BANK], F32, name=f"bank{i}") for i in range(E)]
+
+        nc.vector.memset(wsc[:].bitcast(I32), 0)
+        nc.vector.memset(sc[:].bitcast(I32), 0)
+        wsc_i = wsc[:].bitcast(I32).rearrange("p (e n) -> p e n", e=E)
+
+        def load_scales(engine, n):
+            q = n % 4
+            source = (w4_scales, w8_scales)[n // 4]
+            src = source[:, 0, 4 * q : 4 * q + 4, :].rearrange("e q n -> q e n").bitcast(I32)
+            start = 32 * q + n // 4 * 4
+            engine.dma_start(wsc_i[start : start + 4], src)
+
+
+        raw = []
+        for g in range(2):
+            rows = xT[512 * g : 512 * g + 512, :].rearrange("(p j) w -> p j w", j=PACK)
+            c0 = 0
+            for n, (width, share) in enumerate(CHUNKS[g]):
+                r = keep.tile([P, PACK, width], F32, name=f"raw{g}_{n}")
+                nc.sync.dma_start(r[:], rows[:, :, c0 : c0 + width])
+                raw.append((g, c0, width, share, r))
+                c0 += width
+                if g == 0 and n == 0:
+                    nc.sync.dma_start(offsets[:], offs)
+        nc.sync.dma_start(
+            w4[:].bitcast(I32).rearrange("p (e n) -> p e n", e=E),
+            w4_words.rearrange("e a p n -> p (e a) n").bitcast(I32),
+        )
+        for n in range(6):
+            load_scales(nc.sync, n)
+        nc.sync.dma_start(
+            w8[:].bitcast(I32).rearrange("p (e n) -> p e n", e=E),
+            w8_words.rearrange("e a p n r -> p (e a) (n r)").bitcast(I32),
+        )
+        for n in range(6, 8):
+            load_scales(nc.sync, n)
+        nc.sync.dma_start(bias[:], b)
+        for c0 in (0, T // 2):
+            nc.sync.dma_start(gates[:, c0 : c0 + T // 2], gate[:, c0 : c0 + T // 2])
+
+        def round_part(engine, g, c0, r, lo, hi):
+            dst = xb[g][:, (c0 + lo) * PACK : (c0 + hi) * PACK].rearrange("p (c i t) -> p c t i", i=4, t=PACK)
+            src = r[:, :, lo:hi].rearrange("p t (c i) -> p c t i", i=4)
+            if engine == 0:
+                nc.vector.tensor_copy(dst, src)
+            else:
+                nc.scalar.activation(dst, src, COPY)
+
+        def quantize(g, c0, width):
+            step = min(width, QCOLS)
+            for q in range(c0, c0 + width, step):
+                cols = slice(q, q + step)
+                nc.vector.quantize_mx(
+                    out=words[g][:, cols].bitcast(FP8X4),
+                    scales=sc[4:, cols] if g == 0 else sc[:, cols],
+                    in_=xb[g][:, q * PACK : (q + step) * PACK],
+                )
+
+        def gather_words(g, lo, hi):
+            nc.vector.tensor_copy(gwords[g][:, lo:hi], words[g][:].indirect(offsets[:, lo // 16 : hi // 16]))
+
+        def gather_scales(lo, hi):
+            nc.vector.tensor_copy(gsc[:, lo:hi], sc[:].indirect(offsets[:, lo // 16 : hi // 16]))
+
+        early = list(EARLY)
+        for g, c0, width, share, r in raw:
+            round_part(0, g, c0, r, 0, share)
+            round_part(1, g, c0, r, share, width)
+            if g == 1 and early:
+                gather_words(0, *early.pop(0))
+            quantize(g, c0, width)
+
+        def expert(e):
+            slots = slice(STARTS[e], STARTS[e + 1])
+            w4_e = w4[:, e * N * 2 : (e + 1) * N * 2].bitcast(FP4X4)
+            w8_e = w8[:, e * N * 4 : (e + 1) * N * 4].bitcast(FP8X4)
+            step = BANK if COUNTS[e] == BANK else 128
+            for c in range(0, COUNTS[e], step):
+                cols = slice(STARTS[e] + c, STARTS[e] + c + step)
+                acc = banks[e][:, c : c + step]
+                nc.tensor.matmul_mx(
+                    out=acc, lhsT=w8_e, lhsT_scale=wsc[4:, e * N : (e + 1) * N],
+                    rhs=gwords[0][:, cols].bitcast(FP8X4), rhs_scale=gsc[4:, cols],
+                    start=True, stop=False,
+                )
+                nc.tensor.matmul_mx(
+                    out=acc, lhsT=w4_e, lhsT_scale=wsc[:, e * N : (e + 1) * N],
+                    rhs=gwords[1][:, cols].bitcast(FP8X4), rhs_scale=gsc[:, cols],
+                    start=False, stop=True,
+                )
+            nc.scalar.activation(y[:, slots], banks[e][:, : COUNTS[e]], IDENTITY, bias=bias[:, e : e + 1])
+
+        def scatter(lo, hi):
+            nc.vector.tensor_tensor(
+                win[:].indirect(offsets[:, lo // 16 : hi // 16]), y[:, lo:hi], gates[:, lo:hi], MULT
+            )
+
+        for lo, hi in PIECES:
+            gather_words(1, lo, hi)
+            gather_scales(lo, hi)
+        for e in range(E):
+            expert(e)
+        for lo, hi in SCATTERS:
+            scatter(lo, hi)
+        nc.sync.dma_start(out, win[:])

@@ -24,13 +24,14 @@ IDENTITY = mybir.ActivationFunctionType.Identity
 MULT = mybir.AluOpType.mult
 
 CHUNKS = (
-    ((1024, 576), (512, 224), (512, 272)),
-    ((512, 96), (512, 96), (512, 112), (256, 80), (256, 160)),
+    ((1280, 768), (768, 464)),
+    ((512, 0), (512, 0), (512, 128), (256, 128), (256, 64)),
 )
 QCOLS = 512
-PIECES = ((0, 1024), (1024, 2048))
-SCATTERS = ((0, 768), (768, 1536), (1536, 2048))
-EARLY = ((0, 768), (768, 1536), (1536, 2048))
+PIECES = ((0, 768), (768, 1536), (1792, 2048))
+AHEAD = (1536, 1792)
+SCATTERS = ((0, 768), (768, 2048))
+EARLY = ((0, 1024), (1024, 2048))
 
 
 def tile_moe_rag_lin_bias_kernel(
@@ -53,7 +54,7 @@ def tile_moe_rag_lin_bias_kernel(
         gwords = [keep.tile([P, T], U32, name=f"gwords{g}", align_bytes=64) for g in range(2)]
         xb = [keep.tile([P, T * PACK], BF16, name=f"xb{g}", align_bytes=64) for g in range(2)]
         y = keep.tile([P, T], F32, name="y")
-        win = keep.tile([P, T], F32, name="win")
+        win = keep.tile([P, 2 * T], F32, name="win")
         banks = [psum.tile([P, BANK], F32, name=f"bank{i}") for i in range(E)]
 
         nc.vector.memset(wsc[:].bitcast(I32), 0)
@@ -104,8 +105,8 @@ def tile_moe_rag_lin_bias_kernel(
                 nc.scalar.activation(dst, src, COPY)
 
         def quantize(g, c0, width):
-            step = min(width, QCOLS)
-            for q in range(c0, c0 + width, step):
+            for q in range(c0, c0 + width, QCOLS):
+                step = min(c0 + width - q, QCOLS)
                 cols = slice(q, q + step)
                 nc.vector.quantize_mx(
                     out=words[g][:, cols].bitcast(FP8X4),
@@ -113,19 +114,25 @@ def tile_moe_rag_lin_bias_kernel(
                     in_=xb[g][:, q * PACK : (q + step) * PACK],
                 )
 
-        def gather_words(g, lo, hi):
-            nc.vector.tensor_copy(gwords[g][:, lo:hi], words[g][:].indirect(offsets[:, lo // 16 : hi // 16]))
+        def gather_words(g, lo, hi, tokens=T):
+            nc.vector.tensor_copy(gwords[g][:, lo:hi], words[g][:, :tokens].indirect(offsets[:, lo // 16 : hi // 16]))
 
-        def gather_scales(lo, hi):
-            nc.vector.tensor_copy(gsc[:, lo:hi], sc[:].indirect(offsets[:, lo // 16 : hi // 16]))
+        def gather_scales(lo, hi, tokens=T):
+            nc.vector.tensor_copy(gsc[:, lo:hi], sc[:, :tokens].indirect(offsets[:, lo // 16 : hi // 16]))
 
-        early = list(EARLY)
         for g, c0, width, share, r in raw:
-            round_part(0, g, c0, r, 0, share)
+            last = c0 + width == T
+            if share:
+                round_part(0, g, c0, r, 0, share)
             round_part(1, g, c0, r, share, width)
-            if g == 1 and early:
-                gather_words(0, *early.pop(0))
+            if g == 1 and last:
+                gather_words(1, *AHEAD, tokens=c0)
             quantize(g, c0, width)
+            if g == 1 and last:
+                gather_scales(*AHEAD, tokens=c0)
+            if g == 0 and last:
+                for lo, hi in EARLY:
+                    gather_words(0, lo, hi)
 
         def expert(e):
             slots = slice(STARTS[e], STARTS[e + 1])
@@ -159,4 +166,4 @@ def tile_moe_rag_lin_bias_kernel(
             expert(e)
         for lo, hi in SCATTERS:
             scatter(lo, hi)
-        nc.sync.dma_start(out, win[:])
+        nc.sync.dma_start(out, win[:, :T])

@@ -97,8 +97,8 @@ def tile_moe_rag_lin_bias_kernel(
             nc.sync.dma_start(gates[:, c0 : c0 + T // 2], gate[:, c0 : c0 + T // 2])
 
         def round_part(engine, g, c0, r, lo, hi):
-            dst = xb[g][:, (c0 + lo) * PACK : (c0 + hi) * PACK].rearrange("p (c i t) -> p c t i", i=4, t=PACK)
-            src = r[:, :, lo:hi].rearrange("p t (c i) -> p c t i", i=4)
+            dst = xb[g][:, (c0 + lo) * PACK : (c0 + hi) * PACK].rearrange("p (c i t) -> p c t i", i=2, t=PACK)
+            src = r[:, :, lo:hi].rearrange("p t (c i) -> p c t i", i=2)
             if engine == 0:
                 nc.vector.tensor_copy(dst, src)
             else:

@@ -23,10 +23,9 @@ COPY = mybir.ActivationFunctionType.Copy
 IDENTITY = mybir.ActivationFunctionType.Identity
 MULT = mybir.AluOpType.mult
 
-CHUNKS = (
-    ((1280, 768), (768, 464)),
-    ((512, 0), (512, 0), (512, 128), (256, 128), (256, 64)),
-)
+CHUNKS = ((1280, 768), (512, 512, 512, 256, 256))
+VECTOR_SIXTEENTHS = (8, 7)
+SCALAR_ALONE = 1024
 QCOLS = 512
 PIECES = ((0, 768), (768, 1536), (1792, 2048))
 AHEAD = (1536, 1792)
@@ -73,10 +72,10 @@ def tile_moe_rag_lin_bias_kernel(
         for g in range(2):
             rows = xT[512 * g : 512 * g + 512, :].rearrange("(p j) w -> p j w", j=PACK)
             c0 = 0
-            for n, (width, share) in enumerate(CHUNKS[g]):
+            for n, width in enumerate(CHUNKS[g]):
                 r = keep.tile([P, PACK, width], F32, name=f"raw{g}_{n}")
                 nc.sync.dma_start(r[:], rows[:, :, c0 : c0 + width])
-                raw.append((g, c0, width, share, r))
+                raw.append((g, c0, width, r))
                 c0 += width
                 if g == 0 and n == 0:
                     nc.sync.dma_start(offsets[:], offs)
@@ -104,15 +103,13 @@ def tile_moe_rag_lin_bias_kernel(
             else:
                 nc.scalar.activation(dst, src, COPY)
 
-        def quantize(g, c0, width):
-            for q in range(c0, c0 + width, QCOLS):
-                step = min(c0 + width - q, QCOLS)
-                cols = slice(q, q + step)
-                nc.vector.quantize_mx(
-                    out=words[g][:, cols].bitcast(FP8X4),
-                    scales=sc[4:, cols] if g == 0 else sc[:, cols],
-                    in_=xb[g][:, q * PACK : (q + step) * PACK],
-                )
+        def quantize(g, q, step):
+            cols = slice(q, q + step)
+            nc.vector.quantize_mx(
+                out=words[g][:, cols].bitcast(FP8X4),
+                scales=sc[4:, cols] if g == 0 else sc[:, cols],
+                in_=xb[g][:, q * PACK : (q + step) * PACK],
+            )
 
         def gather_words(g, lo, hi, tokens=T):
             nc.vector.tensor_copy(gwords[g][:, lo:hi], words[g][:, :tokens].indirect(offsets[:, lo // 16 : hi // 16]))
@@ -120,19 +117,22 @@ def tile_moe_rag_lin_bias_kernel(
         def gather_scales(lo, hi, tokens=T):
             nc.vector.tensor_copy(gsc[:, lo:hi], sc[:, :tokens].indirect(offsets[:, lo // 16 : hi // 16]))
 
-        for g, c0, width, share, r in raw:
-            last = c0 + width == T
-            if share:
-                round_part(0, g, c0, r, 0, share)
-            round_part(1, g, c0, r, share, width)
-            if g == 1 and last:
-                gather_words(1, *AHEAD, tokens=c0)
-            quantize(g, c0, width)
-            if g == 1 and last:
-                gather_scales(*AHEAD, tokens=c0)
-            if g == 0 and last:
-                for lo, hi in EARLY:
-                    gather_words(0, lo, hi)
+        for g, c0, width, r in raw:
+            for lo in range(0, width, QCOLS):
+                step = min(width - lo, QCOLS)
+                last = c0 + lo + step == T
+                share = 0 if g == 1 and c0 + lo < SCALAR_ALONE else step * VECTOR_SIXTEENTHS[g] // 16
+                if share:
+                    round_part(0, g, c0, r, lo, lo + share)
+                round_part(1, g, c0, r, lo + share, lo + step)
+                if g == 1 and last:
+                    gather_words(1, *AHEAD, tokens=c0)
+                quantize(g, c0 + lo, step)
+                if g == 1 and last:
+                    gather_scales(*AHEAD, tokens=c0)
+                if g == 0 and last:
+                    for a, z in EARLY:
+                        gather_words(0, a, z)
 
         def expert(e):
             slots = slice(STARTS[e], STARTS[e + 1])

@@ -24,7 +24,7 @@ IDENTITY = mybir.ActivationFunctionType.Identity
 MULT = mybir.AluOpType.mult
 
 CHUNKS = ((1280, 768), (512, 512, 512, 256, 256))
-VECTOR_SIXTEENTHS = (8, 7)
+VECTOR_SIXTEENTHS = (8, 6)
 SCALAR_ALONE = 1024
 QCOLS = 512
 PIECES = ((0, 768), (768, 1536), (1792, 2048))
@@ -121,7 +121,7 @@ def tile_moe_rag_lin_bias_kernel(
             for lo in range(0, width, QCOLS):
                 step = min(width - lo, QCOLS)
                 last = c0 + lo + step == T
-                share = 0 if g == 1 and c0 + lo < SCALAR_ALONE else step * VECTOR_SIXTEENTHS[g] // 16
+                share = 0 if g == 1 and (last or c0 + lo < SCALAR_ALONE) else step * VECTOR_SIXTEENTHS[g] // 16
                 if share:
                     round_part(0, g, c0, r, lo, lo + share)
                 round_part(1, g, c0, r, lo + share, lo + step)

@@ -42,18 +42,18 @@ def tile_moe_rag_lin_bias_kernel(
         psum = ctx.enter_context(tc.psum_pool(name="psum", bufs=1))
 
         offsets = keep.tile([P, T // 16], U16, name="offsets")
-        w8 = keep.tile([P, E * N * 4], U8, name="w8", align_bytes=64)
-        w4 = keep.tile([P, E * N * 2], U8, name="w4", align_bytes=64)
-        wsc = keep.tile([P, E * N], U8, name="wsc", align_bytes=64)
+        w8 = keep.tile([P, E * N * 4], U8, name="w8", align_bytes=256)
+        w4 = keep.tile([P, E * N * 2], U8, name="w4", align_bytes=256)
+        wsc = keep.tile([P, E * N], U8, name="wsc", align_bytes=256)
         bias = keep.tile([P, E], F32, name="bias")
-        gates = keep.tile([P, T], F32, name="gates")
-        sc = keep.tile([P, T], U8, name="sc", align_bytes=64)
-        gsc = keep.tile([P, T], U8, name="gsc", align_bytes=64)
-        words = [keep.tile([P, T], U32, name=f"words{g}", align_bytes=64) for g in range(2)]
-        gwords = [keep.tile([P, T], U32, name=f"gwords{g}", align_bytes=64) for g in range(2)]
-        xb = [keep.tile([P, T * PACK], BF16, name=f"xb{g}", align_bytes=64) for g in range(2)]
-        y = keep.tile([P, T], F32, name="y")
-        win = keep.tile([P, 2 * T], F32, name="win")
+        gates = keep.tile([P, T], F32, name="gates", align_bytes=256)
+        sc = keep.tile([P, T], U8, name="sc", align_bytes=256)
+        gsc = keep.tile([P, T], U8, name="gsc", align_bytes=256)
+        words = [keep.tile([P, T], U32, name=f"words{g}", align_bytes=256) for g in range(2)]
+        gwords = [keep.tile([P, T], U32, name=f"gwords{g}", align_bytes=256) for g in range(2)]
+        xb = [keep.tile([P, T * PACK], BF16, name=f"xb{g}", align_bytes=256) for g in range(2)]
+        y = keep.tile([P, T], F32, name="y", align_bytes=256)
+        win = keep.tile([P, 2 * T], F32, name="win", align_bytes=256)
         banks = [psum.tile([P, BANK], F32, name=f"bank{i}") for i in range(E)]
 
         nc.vector.memset(wsc[:].bitcast(I32), 0)
@@ -73,7 +73,7 @@ def tile_moe_rag_lin_bias_kernel(
             rows = xT[512 * g : 512 * g + 512, :].rearrange("(p j) w -> p j w", j=PACK)
             c0 = 0
             for n, width in enumerate(CHUNKS[g]):
-                r = keep.tile([P, PACK, width], F32, name=f"raw{g}_{n}")
+                r = keep.tile([P, PACK, width], F32, name=f"raw{g}_{n}", align_bytes=256)
                 nc.sync.dma_start(r[:], rows[:, :, c0 : c0 + width])
                 raw.append((g, c0, width, r))
                 c0 += width

@@ -9,7 +9,11 @@ FLOPS = 2 * T * K * N
 
 P = 128
 PACK = 4
+K_PASS = P * PACK
 BANK = 512
+GROUP = 16
+ALIGN = 256
+E4M3_ROW = 4
 
 F32 = mybir.dt.float32
 BF16 = mybir.dt.bfloat16
@@ -24,13 +28,15 @@ IDENTITY = mybir.ActivationFunctionType.Identity
 MULT = mybir.AluOpType.mult
 
 CHUNKS = ((1280, 768), (512, 512, 512, 256, 256))
+BLOCK = 512
 VECTOR_SIXTEENTHS = (8, 6)
 SCALAR_ALONE = 1024
-QCOLS = 512
-PIECES = ((0, 768), (768, 1536), (1792, 2048))
-AHEAD = (1536, 1792)
-SCATTERS = ((0, 768), (768, 2048))
-EARLY = ((0, 1024), (1024, 2048))
+
+LAST_CHUNK = CHUNKS[1][-1]
+AHEAD = (STARTS[E - 1], T - LAST_CHUNK)
+FIRST = STARTS[5]
+PIECES = ((0, FIRST), (FIRST, AHEAD[0]), (AHEAD[1], T))
+SCATTERS = ((0, FIRST), (FIRST, T))
 
 
 def tile_moe_rag_lin_bias_kernel(
@@ -41,129 +47,114 @@ def tile_moe_rag_lin_bias_kernel(
         keep = ctx.enter_context(tc.tile_pool(name="keep", bufs=1))
         psum = ctx.enter_context(tc.psum_pool(name="psum", bufs=1))
 
-        offsets = keep.tile([P, T // 16], U16, name="offsets")
-        w8 = keep.tile([P, E * N * 4], U8, name="w8", align_bytes=256)
-        w4 = keep.tile([P, E * N * 2], U8, name="w4", align_bytes=256)
-        wsc = keep.tile([P, E * N], U8, name="wsc", align_bytes=256)
+        offsets = keep.tile([P, T // GROUP], U16, name="offsets")
+        w8 = keep.tile([P, E * N * 4], U8, name="w8", align_bytes=ALIGN)
+        w4 = keep.tile([P, E * N * 2], U8, name="w4", align_bytes=ALIGN)
+        weight_scales = keep.tile([P, E * N], U8, name="weight_scales", align_bytes=ALIGN)
         bias = keep.tile([P, E], F32, name="bias")
-        gates = keep.tile([P, T], F32, name="gates", align_bytes=256)
-        sc = keep.tile([P, T], U8, name="sc", align_bytes=256)
-        gsc = keep.tile([P, T], U8, name="gsc", align_bytes=256)
-        words = [keep.tile([P, T], U32, name=f"words{g}", align_bytes=256) for g in range(2)]
-        gwords = [keep.tile([P, T], U32, name=f"gwords{g}", align_bytes=256) for g in range(2)]
-        xb = [keep.tile([P, T * PACK], BF16, name=f"xb{g}", align_bytes=256) for g in range(2)]
-        y = keep.tile([P, T], F32, name="y", align_bytes=256)
-        win = keep.tile([P, 2 * T], F32, name="win", align_bytes=256)
-        banks = [psum.tile([P, BANK], F32, name=f"bank{i}") for i in range(E)]
+        gates = keep.tile([P, T], F32, name="gates", align_bytes=ALIGN)
+        token_scales = keep.tile([P, T], U8, name="token_scales", align_bytes=ALIGN)
+        slot_scales = keep.tile([P, T], U8, name="slot_scales", align_bytes=ALIGN)
+        token_words = [keep.tile([P, T], U32, name=f"token_words{g}", align_bytes=ALIGN) for g in range(2)]
+        slot_words = [keep.tile([P, T], U32, name=f"slot_words{g}", align_bytes=ALIGN) for g in range(2)]
+        rounded = [keep.tile([P, T * PACK], BF16, name=f"rounded{g}", align_bytes=ALIGN) for g in range(2)]
+        y = keep.tile([P, T], F32, name="y", align_bytes=ALIGN)
+        window = keep.tile([P, 2 * T], F32, name="window", align_bytes=ALIGN)
+        banks = [psum.tile([P, BANK], F32, name=f"bank{e}") for e in range(E)]
 
-        nc.vector.memset(wsc[:].bitcast(I32), 0)
-        nc.vector.memset(sc[:].bitcast(I32), 0)
-        wsc_i = wsc[:].bitcast(I32).rearrange("p (e n) -> p e n", e=E)
+        nc.vector.memset(weight_scales[:].bitcast(I32), 0)
+        nc.vector.memset(token_scales[:].bitcast(I32), 0)
 
-        def load_scales(engine, n):
-            q = n % 4
-            source = (w4_scales, w8_scales)[n // 4]
-            src = source[:, 0, 4 * q : 4 * q + 4, :].rearrange("e q n -> q e n").bitcast(I32)
-            start = 32 * q + n // 4 * 4
-            engine.dma_start(wsc_i[start : start + 4], src)
-
-
-        raw = []
+        chunks = []
         for g in range(2):
-            rows = xT[512 * g : 512 * g + 512, :].rearrange("(p j) w -> p j w", j=PACK)
+            rows = xT[K_PASS * g : K_PASS * (g + 1), :].rearrange("(p j) w -> p j w", j=PACK)
             c0 = 0
             for n, width in enumerate(CHUNKS[g]):
-                r = keep.tile([P, PACK, width], F32, name=f"raw{g}_{n}", align_bytes=256)
-                nc.sync.dma_start(r[:], rows[:, :, c0 : c0 + width])
-                raw.append((g, c0, width, r))
-                c0 += width
-                if g == 0 and n == 0:
+                raw = keep.tile([P, PACK, width], F32, name=f"raw{g}_{n}", align_bytes=ALIGN)
+                nc.sync.dma_start(raw[:], rows[:, :, c0 : c0 + width])
+                if not chunks:
                     nc.sync.dma_start(offsets[:], offs)
-        nc.sync.dma_start(
-            w4[:].bitcast(I32).rearrange("p (e n) -> p e n", e=E),
-            w4_words.rearrange("e a p n -> p (e a) n").bitcast(I32),
-        )
-        for n in range(6):
-            load_scales(nc.sync, n)
-        nc.sync.dma_start(
-            w8[:].bitcast(I32).rearrange("p (e n) -> p e n", e=E),
-            w8_words.rearrange("e a p n r -> p (e a) (n r)").bitcast(I32),
-        )
-        for n in range(6, 8):
-            load_scales(nc.sync, n)
+                chunks.append((g, c0, width, raw))
+                c0 += width
+
+        def load_weights(tile, words, scales, first_row):
+            nc.sync.dma_start(tile[:].bitcast(I32).rearrange("p (e n) -> p e n", e=E), words.bitcast(I32))
+            planes = weight_scales[:].bitcast(I32).rearrange("p (e n) -> p e n", e=E)
+            for quadrant in range(4):
+                start = 32 * quadrant + first_row
+                source = scales[:, 0, 4 * quadrant : 4 * quadrant + 4, :].rearrange("e q n -> q e n")
+                nc.sync.dma_start(planes[start : start + 4], source.bitcast(I32))
+
+        load_weights(w4, w4_words.rearrange("e a p n -> p (e a) n"), w4_scales, 0)
+        load_weights(w8, w8_words.rearrange("e a p n r -> p (e a) (n r)"), w8_scales, E4M3_ROW)
         nc.sync.dma_start(bias[:], b)
-        for c0 in (0, T // 2):
-            nc.sync.dma_start(gates[:, c0 : c0 + T // 2], gate[:, c0 : c0 + T // 2])
+        for lo, hi in SCATTERS:
+            nc.sync.dma_start(gates[:, lo:hi], gate[:, lo:hi])
 
-        def round_part(engine, g, c0, r, lo, hi):
-            dst = xb[g][:, (c0 + lo) * PACK : (c0 + hi) * PACK].rearrange("p (c i t) -> p c t i", i=2, t=PACK)
-            src = r[:, :, lo:hi].rearrange("p t (c i) -> p c t i", i=2)
-            if engine == 0:
-                nc.vector.tensor_copy(dst, src)
-            else:
-                nc.scalar.activation(dst, src, COPY)
+        def rounding_views(g, c0, raw, lo, hi):
+            dst = rounded[g][:, (c0 + lo) * PACK : (c0 + hi) * PACK].rearrange("p (c i t) -> p c t i", i=2, t=PACK)
+            return dst, raw[:, :, lo:hi].rearrange("p t (c i) -> p c t i", i=2)
 
-        def quantize(g, q, step):
-            cols = slice(q, q + step)
+        def quantize(g, lo, hi):
             nc.vector.quantize_mx(
-                out=words[g][:, cols].bitcast(FP8X4),
-                scales=sc[4:, cols] if g == 0 else sc[:, cols],
-                in_=xb[g][:, q * PACK : (q + step) * PACK],
+                out=token_words[g][:, lo:hi].bitcast(FP8X4),
+                scales=token_scales[E4M3_ROW:, lo:hi] if g == 0 else token_scales[:, lo:hi],
+                in_=rounded[g][:, lo * PACK : hi * PACK],
             )
 
+        def entries(lo, hi):
+            return offsets[:, lo // GROUP : hi // GROUP]
+
         def gather_words(g, lo, hi, tokens=T):
-            nc.vector.tensor_copy(gwords[g][:, lo:hi], words[g][:, :tokens].indirect(offsets[:, lo // 16 : hi // 16]))
+            nc.vector.tensor_copy(slot_words[g][:, lo:hi], token_words[g][:, :tokens].indirect(entries(lo, hi)))
 
         def gather_scales(lo, hi, tokens=T):
-            nc.vector.tensor_copy(gsc[:, lo:hi], sc[:, :tokens].indirect(offsets[:, lo // 16 : hi // 16]))
+            nc.vector.tensor_copy(slot_scales[:, lo:hi], token_scales[:, :tokens].indirect(entries(lo, hi)))
 
-        for g, c0, width, r in raw:
-            for lo in range(0, width, QCOLS):
-                step = min(width - lo, QCOLS)
-                last = c0 + lo + step == T
-                share = 0 if g == 1 and (last or c0 + lo < SCALAR_ALONE) else step * VECTOR_SIXTEENTHS[g] // 16
-                if share:
-                    round_part(0, g, c0, r, lo, lo + share)
-                round_part(1, g, c0, r, lo + share, lo + step)
+        for g, c0, width, raw in chunks:
+            for lo in range(0, width, BLOCK):
+                hi = min(lo + BLOCK, width)
+                last = c0 + hi == T
+                split = lo
+                if g == 0 or not (last or c0 + lo < SCALAR_ALONE):
+                    split = lo + (hi - lo) * VECTOR_SIXTEENTHS[g] // 16
+                    nc.vector.tensor_copy(*rounding_views(g, c0, raw, lo, split))
+                nc.scalar.activation(*rounding_views(g, c0, raw, split, hi), COPY)
                 if g == 1 and last:
                     gather_words(1, *AHEAD, tokens=c0)
-                quantize(g, c0 + lo, step)
+                quantize(g, c0 + lo, c0 + hi)
                 if g == 1 and last:
                     gather_scales(*AHEAD, tokens=c0)
                 if g == 0 and last:
-                    for a, z in EARLY:
-                        gather_words(0, a, z)
-
-        def expert(e):
-            slots = slice(STARTS[e], STARTS[e + 1])
-            w4_e = w4[:, e * N * 2 : (e + 1) * N * 2].bitcast(FP4X4)
-            w8_e = w8[:, e * N * 4 : (e + 1) * N * 4].bitcast(FP8X4)
-            step = BANK if COUNTS[e] == BANK else 128
-            for c in range(0, COUNTS[e], step):
-                cols = slice(STARTS[e] + c, STARTS[e] + c + step)
-                acc = banks[e][:, c : c + step]
-                nc.tensor.matmul_mx(
-                    out=acc, lhsT=w8_e, lhsT_scale=wsc[4:, e * N : (e + 1) * N],
-                    rhs=gwords[0][:, cols].bitcast(FP8X4), rhs_scale=gsc[4:, cols],
-                    start=True, stop=False,
-                )
-                nc.tensor.matmul_mx(
-                    out=acc, lhsT=w4_e, lhsT_scale=wsc[:, e * N : (e + 1) * N],
-                    rhs=gwords[1][:, cols].bitcast(FP8X4), rhs_scale=gsc[:, cols],
-                    start=False, stop=True,
-                )
-            nc.scalar.activation(y[:, slots], banks[e][:, : COUNTS[e]], IDENTITY, bias=bias[:, e : e + 1])
-
-        def scatter(lo, hi):
-            nc.vector.tensor_tensor(
-                win[:].indirect(offsets[:, lo // 16 : hi // 16]), y[:, lo:hi], gates[:, lo:hi], MULT
-            )
+                    gather_words(0, 0, T // 2)
+                    gather_words(0, T // 2, T)
 
         for lo, hi in PIECES:
             gather_words(1, lo, hi)
             gather_scales(lo, hi)
+
         for e in range(E):
-            expert(e)
+            columns = slice(e * N, (e + 1) * N)
+            w8_e = w8[:, e * N * 4 : (e + 1) * N * 4].bitcast(FP8X4)
+            w4_e = w4[:, e * N * 2 : (e + 1) * N * 2].bitcast(FP4X4)
+            step = BANK if COUNTS[e] == BANK else 128
+            for c in range(0, COUNTS[e], step):
+                slots = slice(STARTS[e] + c, STARTS[e] + c + step)
+                acc = banks[e][:, c : c + step]
+                nc.tensor.matmul_mx(
+                    out=acc, lhsT=w8_e, lhsT_scale=weight_scales[E4M3_ROW:, columns],
+                    rhs=slot_words[0][:, slots].bitcast(FP8X4), rhs_scale=slot_scales[E4M3_ROW:, slots],
+                    start=True, stop=False,
+                )
+                nc.tensor.matmul_mx(
+                    out=acc, lhsT=w4_e, lhsT_scale=weight_scales[:, columns],
+                    rhs=slot_words[1][:, slots].bitcast(FP8X4), rhs_scale=slot_scales[:, slots],
+                    start=False, stop=True,
+                )
+            nc.scalar.activation(
+                y[:, STARTS[e] : STARTS[e + 1]], banks[e][:, : COUNTS[e]], IDENTITY, bias=bias[:, e : e + 1]
+            )
+
         for lo, hi in SCATTERS:
-            scatter(lo, hi)
-        nc.sync.dma_start(out, win[:, :T])
+            nc.vector.tensor_tensor(window[:].indirect(entries(lo, hi)), y[:, lo:hi], gates[:, lo:hi], MULT)
+        nc.sync.dma_start(out, window[:, :T])

@@ -27,12 +27,12 @@ COPY = mybir.ActivationFunctionType.Copy
 IDENTITY = mybir.ActivationFunctionType.Identity
 MULT = mybir.AluOpType.mult
 
-CHUNKS = ((1280, 768), (512, 512, 512, 256, 256))
+CHUNKS = ((1280,768,), (512,512,512,256,256,))
 BLOCK = 512
-VECTOR_SIXTEENTHS = (8, 6)
-SCALAR_ALONE = 1024
+VECTOR_COLUMNS = ((512, 128, 0, 384, 0,), (0, 0, 192, 96, 0,))
+BORDERS = ((512, 1024, 1280, 1792, 2048,), (512, 1024, 1536, 1792, 2048,))
 
-LAST_CHUNK = CHUNKS[1][-1]
+LAST_CHUNK = 256
 AHEAD = (STARTS[E - 1], T - LAST_CHUNK)
 FIRST = STARTS[5]
 PIECES = ((0, FIRST), (FIRST, AHEAD[0]), (AHEAD[1], T))
@@ -55,7 +55,7 @@ def tile_moe_rag_lin_bias_kernel(
         gates = keep.tile([P, T], F32, name="gates", align_bytes=ALIGN)
         token_scales = keep.tile([P, T], U8, name="token_scales", align_bytes=ALIGN)
         slot_scales = keep.tile([P, T], U8, name="slot_scales", align_bytes=ALIGN)
-        token_words = [keep.tile([P, T], U32, name=f"token_words{g}", align_bytes=ALIGN) for g in range(2)]
+        token_words = [keep.tile([P, (2 - g) * T], U32, name=f"token_words{g}", align_bytes=ALIGN) for g in range(2)]
         slot_words = [keep.tile([P, T], U32, name=f"slot_words{g}", align_bytes=ALIGN) for g in range(2)]
         rounded = [keep.tile([P, T * PACK], BF16, name=f"rounded{g}", align_bytes=ALIGN) for g in range(2)]
         y = keep.tile([P, T], F32, name="y", align_bytes=ALIGN)
@@ -111,27 +111,33 @@ def tile_moe_rag_lin_bias_kernel(
         def gather_scales(lo, hi, tokens=T):
             nc.vector.tensor_copy(slot_scales[:, lo:hi], token_scales[:, :tokens].indirect(entries(lo, hi)))
 
+        blocks = [0, 0]
+        done = [0, 0]
         for g, c0, width, raw in chunks:
-            for lo in range(0, width, BLOCK):
-                hi = min(lo + BLOCK, width)
+            ends = [end - c0 for end in BORDERS[g] if c0 < end < c0 + width] + [width]
+            for lo, hi in zip([0] + ends, ends):
                 last = c0 + hi == T
-                split = lo
-                if g == 0 or not (last or c0 + lo < SCALAR_ALONE):
-                    split = lo + (hi - lo) * VECTOR_SIXTEENTHS[g] // 16
+                split = lo + VECTOR_COLUMNS[g][blocks[g]]
+                blocks[g] = blocks[g] + 1
+                if split > lo:
                     nc.vector.tensor_copy(*rounding_views(g, c0, raw, lo, split))
-                nc.scalar.activation(*rounding_views(g, c0, raw, split, hi), COPY)
+                if split < hi:
+                    nc.scalar.activation(*rounding_views(g, c0, raw, split, hi), COPY)
+                if c0 + hi not in BORDERS[g]:
+                    continue
                 if g == 1 and last:
-                    gather_words(1, *AHEAD, tokens=c0)
-                quantize(g, c0 + lo, c0 + hi)
+                    gather_words(1, *AHEAD, tokens=AHEAD[1])
+                quantize(g, done[g], c0 + hi)
+                done[g] = c0 + hi
                 if g == 1 and last:
-                    gather_scales(*AHEAD, tokens=c0)
+                    gather_scales(*AHEAD, tokens=AHEAD[1])
                 if g == 0 and last:
-                    gather_words(0, 0, T // 2)
-                    gather_words(0, T // 2, T)
+                    gather_words(0, 0, T, tokens=2 * T)
 
+        gather_scales(0, AHEAD[0])
         for lo, hi in PIECES:
             gather_words(1, lo, hi)
-            gather_scales(lo, hi)
+        gather_scales(AHEAD[1], T)
 
         for e in range(E):
             columns = slice(e * N, (e + 1) * N)

@@ -134,10 +134,9 @@ def tile_moe_rag_lin_bias_kernel(
                 if g == 0 and last:
                     gather_words(0, 0, T, tokens=2 * T)
 
-        gather_scales(0, AHEAD[0])
         for lo, hi in PIECES:
             gather_words(1, lo, hi)
-        gather_scales(AHEAD[1], T)
+            gather_scales(lo, hi)
 
         for e in range(E):
             columns = slice(e * N, (e + 1) * N)

@@ -77,17 +77,27 @@ def tile_moe_rag_lin_bias_kernel(
                 chunks.append((g, c0, width, raw))
                 c0 += width
 
-        def load_weights(tile, words, scales, first_row):
-            nc.sync.dma_start(tile[:].bitcast(I32).rearrange("p (e n) -> p e n", e=E), words.bitcast(I32))
+        def load_words(tile, words, lo, hi):
+            view = tile[:].bitcast(I32).rearrange("p (e n) -> p e n", e=E)
+            nc.sync.dma_start(view[:, lo:hi], words.bitcast(I32)[:, lo:hi])
+
+        def load_scales(quadrant):
             planes = weight_scales[:].bitcast(I32).rearrange("p (e n) -> p e n", e=E)
-            for quadrant in range(4):
+            for scales, first_row in ((w8_scales, E4M3_ROW), (w4_scales, 0)):
                 start = 32 * quadrant + first_row
                 source = scales[:, 0, 4 * quadrant : 4 * quadrant + 4, :].rearrange("e q n -> q e n")
                 nc.sync.dma_start(planes[start : start + 4], source.bitcast(I32))
 
-        load_weights(w4, w4_words.rearrange("e a p n -> p (e a) n"), w4_scales, 0)
-        load_weights(w8, w8_words.rearrange("e a p n r -> p (e a) (n r)"), w8_scales, E4M3_ROW)
+        words8 = w8_words.rearrange("e a p n r -> p (e a) (n r)")
+        words4 = w4_words.rearrange("e a p n -> p (e a) n")
+        load_scales(0)
+        load_words(w8, words8, 0, 5)
+        load_words(w4, words4, 0, 5)
+        for quadrant in range(1, 4):
+            load_scales(quadrant)
         nc.sync.dma_start(bias[:], b)
+        load_words(w8, words8, 5, E)
+        load_words(w4, words4, 5, E)
         for lo, hi in SCATTERS:
             nc.sync.dma_start(gates[:, lo:hi], gate[:, lo:hi])
 

@@ -27,10 +27,46 @@ COPY = mybir.ActivationFunctionType.Copy
 IDENTITY = mybir.ActivationFunctionType.Identity
 MULT = mybir.AluOpType.mult
 
-CHUNKS = ((1280,768,), (512,512,512,256,256,))
-BLOCK = 512
-VECTOR_COLUMNS = ((512, 128, 0, 384, 0,), (0, 0, 192, 96, 0,))
-BORDERS = ((512, 1024, 1280, 1792, 2048,), (512, 1024, 1536, 1792, 2048,))
+LOADS = (
+    (0, 0, 4, 0, 1280, 0, 1280),
+    (0, 0, 4, 1280, 2048, 1280, 2048),
+    (1, 0, 4, 0, 512, 0, 512),
+    (1, 0, 4, 512, 1024, 512, 1024),
+    (1, 0, 4, 1024, 1536, 1024, 1536),
+    (1, 0, 4, 1536, 1792, 1536, 1792),
+    (1, 0, 4, 1792, 2048, 1792, 2048),
+)
+LIST_BEHIND = 0
+WORK = (
+    ("V", 0, 0, 512, 0),
+    ("Q", 0, 0, 512, 0),
+    ("V", 0, 512, 640, 0),
+    ("S", 0, 640, 1024, 0),
+    ("Q", 0, 512, 1024, 0),
+    ("S", 0, 1024, 1280, 0),
+    ("Q", 0, 1024, 1280, 0),
+    ("V", 0, 1280, 1664, 0),
+    ("S", 0, 1664, 1792, 0),
+    ("Q", 0, 1280, 1792, 0),
+    ("S", 0, 1792, 2048, 0),
+    ("Q", 0, 1792, 2048, 0),
+    ("W", 0, 0, 2048, 4096),
+    ("S", 1, 0, 512, 0),
+    ("Q", 1, 0, 512, 0),
+    ("S", 1, 512, 1024, 0),
+    ("Q", 1, 512, 1024, 0),
+    ("V", 1, 1024, 1216, 0),
+    ("S", 1, 1216, 1536, 0),
+    ("Q", 1, 1024, 1536, 0),
+    ("V", 1, 1536, 1600, 0),
+    ("S", 1, 1600, 1792, 0),
+    ("Q", 1, 1536, 1792, 0),
+    ("V", 1, 1792, 1856, 0),
+    ("S", 1, 1856, 2048, 0),
+    ("W", 1, 1536, 1792, 1792),
+    ("Q", 1, 1792, 2048, 0),
+    ("B", 1, 1536, 1792, 1792),
+)
 
 LAST_CHUNK = 256
 AHEAD = (STARTS[E - 1], T - LAST_CHUNK)
@@ -54,7 +90,6 @@ def tile_moe_rag_lin_bias_kernel(
         bias = keep.tile([P, E], F32, name="bias")
         gates = keep.tile([P, T], F32, name="gates", align_bytes=ALIGN)
         token_scales = keep.tile([P, T], U8, name="token_scales", align_bytes=ALIGN)
-        slot_scales = keep.tile([P, T], U8, name="slot_scales", align_bytes=ALIGN)
         token_words = [keep.tile([P, (2 - g) * T], U32, name=f"token_words{g}", align_bytes=ALIGN) for g in range(2)]
         slot_words = [keep.tile([P, T], U32, name=f"slot_words{g}", align_bytes=ALIGN) for g in range(2)]
         rounded = [keep.tile([P, T * PACK], BF16, name=f"rounded{g}", align_bytes=ALIGN) for g in range(2)]
@@ -65,17 +100,14 @@ def tile_moe_rag_lin_bias_kernel(
         nc.vector.memset(weight_scales[:].bitcast(I32), 0)
         nc.vector.memset(token_scales[:].bitcast(I32), 0)
 
-        chunks = []
-        for g in range(2):
+        raws = {}
+        for n, (g, r0, r1, c0, c1, t0, t1) in enumerate(LOADS):
             rows = xT[K_PASS * g : K_PASS * (g + 1), :].rearrange("(p j) w -> p j w", j=PACK)
-            c0 = 0
-            for n, width in enumerate(CHUNKS[g]):
-                raw = keep.tile([P, PACK, width], F32, name=f"raw{g}_{n}", align_bytes=ALIGN)
-                nc.sync.dma_start(raw[:], rows[:, :, c0 : c0 + width])
-                if not chunks:
-                    nc.sync.dma_start(offsets[:], offs)
-                chunks.append((g, c0, width, raw))
-                c0 += width
+            if (g, t0, t1) not in raws:
+                raws[(g, t0, t1)] = keep.tile([P, PACK, t1 - t0], F32, name=f"raw{g}_{t0}", tag=f"raw{g}_{t0}", align_bytes=ALIGN)
+            nc.sync.dma_start(raws[(g, t0, t1)][:, r0:r1, c0 - t0 : c1 - t0], rows[:, r0:r1, c0:c1])
+            if n == LIST_BEHIND:
+                nc.sync.dma_start(offsets[:], offs)
 
         def load_words(tile, words, lo, hi):
             view = tile[:].bitcast(I32).rearrange("p (e n) -> p e n", e=E)
@@ -101,9 +133,10 @@ def tile_moe_rag_lin_bias_kernel(
         for lo, hi in SCATTERS:
             nc.sync.dma_start(gates[:, lo:hi], gate[:, lo:hi])
 
-        def rounding_views(g, c0, raw, lo, hi):
-            dst = rounded[g][:, (c0 + lo) * PACK : (c0 + hi) * PACK].rearrange("p (c i t) -> p c t i", i=2, t=PACK)
-            return dst, raw[:, :, lo:hi].rearrange("p t (c i) -> p c t i", i=2)
+        def rounding_views(g, lo, hi):
+            raw, t0 = [(tile, key[1]) for key, tile in raws.items() if key[0] == g and key[1] <= lo and hi <= key[2]][0]
+            dst = rounded[g][:, lo * PACK : hi * PACK].rearrange("p (c i t) -> p c t i", i=2, t=PACK)
+            return dst, raw[:, :, lo - t0 : hi - t0].rearrange("p t (c i) -> p c t i", i=2)
 
         def quantize(g, lo, hi):
             nc.vector.quantize_mx(
@@ -119,35 +152,28 @@ def tile_moe_rag_lin_bias_kernel(
             nc.vector.tensor_copy(slot_words[g][:, lo:hi], token_words[g][:, :tokens].indirect(entries(lo, hi)))
 
         def gather_scales(lo, hi, tokens=T):
-            nc.vector.tensor_copy(slot_scales[:, lo:hi], token_scales[:, :tokens].indirect(entries(lo, hi)))
+            nc.vector.tensor_copy(late[0][:, lo:hi], token_scales[:, :tokens].indirect(entries(lo, hi)))
 
-        blocks = [0, 0]
-        done = [0, 0]
-        for g, c0, width, raw in chunks:
-            ends = [end - c0 for end in BORDERS[g] if c0 < end < c0 + width] + [width]
-            for lo, hi in zip([0] + ends, ends):
-                last = c0 + hi == T
-                split = lo + VECTOR_COLUMNS[g][blocks[g]]
-                blocks[g] = blocks[g] + 1
-                if split > lo:
-                    nc.vector.tensor_copy(*rounding_views(g, c0, raw, lo, split))
-                if split < hi:
-                    nc.scalar.activation(*rounding_views(g, c0, raw, split, hi), COPY)
-                if c0 + hi not in BORDERS[g]:
-                    continue
-                if g == 1 and last:
-                    gather_words(1, *AHEAD, tokens=AHEAD[1])
-                quantize(g, done[g], c0 + hi)
-                done[g] = c0 + hi
-                if g == 1 and last:
-                    gather_scales(*AHEAD, tokens=AHEAD[1])
-                if g == 0 and last:
-                    gather_words(0, 0, T, tokens=2 * T)
+        late = []
+        for kind, g, lo, hi, tokens in WORK:
+            if kind == "B":
+                late.append(keep.tile([P, T], U8, name="slot_scales", tag=f"raw1_{AHEAD[1]}", align_bytes=ALIGN))
+            if kind == "V":
+                nc.vector.tensor_copy(*rounding_views(g, lo, hi))
+            if kind == "S":
+                nc.scalar.activation(*rounding_views(g, lo, hi), COPY)
+            if kind == "Q":
+                quantize(g, lo, hi)
+            if kind == "W":
+                gather_words(g, lo, hi, tokens)
+            if kind == "B":
+                gather_scales(lo, hi, tokens)
 
         for lo, hi in PIECES:
             gather_words(1, lo, hi)
             gather_scales(lo, hi)
 
+        slot_scales = late[0]
         for e in range(E):
             columns = slice(e * N, (e + 1) * N)
             w8_e = w8[:, e * N * 4 : (e + 1) * N * 4].bitcast(FP8X4)

@@ -58,11 +58,11 @@ WORK = (
     ("V", 1, 1024, 1216, 0),
     ("S", 1, 1216, 1536, 0),
     ("Q", 1, 1024, 1536, 0),
-    ("V", 1, 1536, 1600, 0),
-    ("S", 1, 1600, 1792, 0),
+    ("V", 1, 1536, 1632, 0),
+    ("S", 1, 1632, 1792, 0),
     ("Q", 1, 1536, 1792, 0),
-    ("V", 1, 1792, 1856, 0),
-    ("S", 1, 1856, 2048, 0),
+    ("V", 1, 1792, 1888, 0),
+    ("S", 1, 1888, 2048, 0),
     ("W", 1, 1536, 1792, 1792),
     ("Q", 1, 1792, 2048, 0),
     ("B", 1, 1536, 1792, 1792),

@@ -14,6 +14,8 @@ BANK = 512
 GROUP = 16
 ALIGN = 256
 E4M3_ROW = 4
+BLOCK = 512
+WIDE = 256
 
 F32 = mybir.dt.float32
 BF16 = mybir.dt.bfloat16
@@ -24,55 +26,20 @@ U8 = mybir.dt.uint8
 FP8X4 = mybir.dt.float8_e4m3fn_x4
 FP4X4 = mybir.dt.float4_e2m1fn_x4
 COPY = mybir.ActivationFunctionType.Copy
-IDENTITY = mybir.ActivationFunctionType.Identity
+ADD = mybir.AluOpType.add
 MULT = mybir.AluOpType.mult
 
-LOADS = (
-    (0, 0, 4, 0, 1280, 0, 1280),
-    (0, 0, 4, 1280, 2048, 1280, 2048),
-    (1, 0, 4, 0, 512, 0, 512),
-    (1, 0, 4, 512, 1024, 512, 1024),
-    (1, 0, 4, 1024, 1536, 1024, 1536),
-    (1, 0, 4, 1536, 1792, 1536, 1792),
-    (1, 0, 4, 1792, 2048, 1792, 2048),
+CHUNKS = (
+    ((0, 1280, 640), (1280, 2048, 384)),
+    ((0, 512, 0), (512, 1024, 0), (1024, 1536, 192), (1536, 1792, 96), (1792, 2048, 96)),
 )
-LIST_BEHIND = 0
-WORK = (
-    ("V", 0, 0, 512, 0),
-    ("Q", 0, 0, 512, 0),
-    ("V", 0, 512, 640, 0),
-    ("S", 0, 640, 1024, 0),
-    ("Q", 0, 512, 1024, 0),
-    ("S", 0, 1024, 1280, 0),
-    ("Q", 0, 1024, 1280, 0),
-    ("V", 0, 1280, 1664, 0),
-    ("S", 0, 1664, 1792, 0),
-    ("Q", 0, 1280, 1792, 0),
-    ("S", 0, 1792, 2048, 0),
-    ("Q", 0, 1792, 2048, 0),
-    ("W", 0, 0, 2048, 4096),
-    ("S", 1, 0, 512, 0),
-    ("Q", 1, 0, 512, 0),
-    ("S", 1, 512, 1024, 0),
-    ("Q", 1, 512, 1024, 0),
-    ("V", 1, 1024, 1216, 0),
-    ("S", 1, 1216, 1536, 0),
-    ("Q", 1, 1024, 1536, 0),
-    ("V", 1, 1536, 1632, 0),
-    ("S", 1, 1632, 1792, 0),
-    ("Q", 1, 1536, 1792, 0),
-    ("V", 1, 1792, 1888, 0),
-    ("S", 1, 1888, 2048, 0),
-    ("W", 1, 1536, 1792, 1792),
-    ("Q", 1, 1792, 2048, 0),
-    ("B", 1, 1536, 1792, 1792),
-)
-
 LAST_CHUNK = 256
 AHEAD = (STARTS[E - 1], T - LAST_CHUNK)
-FIRST = STARTS[5]
-PIECES = ((0, FIRST), (FIRST, AHEAD[0]), (AHEAD[1], T))
-SCATTERS = ((0, FIRST), (FIRST, T))
+PIECES = (AHEAD, (0, 384), (384, 768), (768, 1152), (1152, 1536), (AHEAD[1], T))
+
+
+def runs(lo, hi):
+    return [(e, max(lo, STARTS[e]), min(hi, STARTS[e + 1])) for e in range(E) if STARTS[e] < hi and lo < STARTS[e + 1]]
 
 
 def tile_moe_rag_lin_bias_kernel(
@@ -91,52 +58,55 @@ def tile_moe_rag_lin_bias_kernel(
         gates = keep.tile([P, T], F32, name="gates", align_bytes=ALIGN)
         token_scales = keep.tile([P, T], U8, name="token_scales", align_bytes=ALIGN)
         token_words = [keep.tile([P, (2 - g) * T], U32, name=f"token_words{g}", align_bytes=ALIGN) for g in range(2)]
-        slot_words = [keep.tile([P, T], U32, name=f"slot_words{g}", align_bytes=ALIGN) for g in range(2)]
+        first_words = keep.tile([P, T], U32, name="first_words", align_bytes=ALIGN)
         rounded = [keep.tile([P, T * PACK], BF16, name=f"rounded{g}", align_bytes=ALIGN) for g in range(2)]
         y = keep.tile([P, T], F32, name="y", align_bytes=ALIGN)
-        window = keep.tile([P, 2 * T], F32, name="window", align_bytes=ALIGN)
-        banks = [psum.tile([P, BANK], F32, name=f"bank{e}") for e in range(E)]
+        window = keep.tile([P, T], F32, name="window", align_bytes=ALIGN)
+        banks = [psum.tile([P, BANK], F32, name=f"bank{i}") for i in range(len(PIECES))]
 
         nc.vector.memset(weight_scales[:].bitcast(I32), 0)
         nc.vector.memset(token_scales[:].bitcast(I32), 0)
 
         raws = {}
-        for n, (g, r0, r1, c0, c1, t0, t1) in enumerate(LOADS):
+        for g in range(2):
             rows = xT[K_PASS * g : K_PASS * (g + 1), :].rearrange("(p j) w -> p j w", j=PACK)
-            if (g, t0, t1) not in raws:
-                raws[(g, t0, t1)] = keep.tile([P, PACK, t1 - t0], F32, name=f"raw{g}_{t0}", tag=f"raw{g}_{t0}", align_bytes=ALIGN)
-            nc.sync.dma_start(raws[(g, t0, t1)][:, r0:r1, c0 - t0 : c1 - t0], rows[:, r0:r1, c0:c1])
-            if n == LIST_BEHIND:
-                nc.sync.dma_start(offsets[:], offs)
+            for lo, hi, share in CHUNKS[g]:
+                raws[g, lo] = keep.tile([P, PACK, hi - lo], F32, name=f"raw{g}_{lo}", tag=f"raw{g}_{lo}", align_bytes=ALIGN)
+                nc.sync.dma_start(raws[g, lo][:], rows[:, :, lo:hi])
+                if (g, lo) == (0, 0):
+                    nc.sync.dma_start(offsets[:], offs)
 
-        def load_words(tile, words, lo, hi):
-            view = tile[:].bitcast(I32).rearrange("p (e n) -> p e n", e=E)
-            nc.sync.dma_start(view[:, lo:hi], words.bitcast(I32)[:, lo:hi])
+        words8 = w8_words.rearrange("e a p n r -> p (e a) (n r)")
+        words4 = w4_words.rearrange("e a p n -> p (e a) n")
 
-        def load_scales(quadrant):
-            planes = weight_scales[:].bitcast(I32).rearrange("p (e n) -> p e n", e=E)
+        def load_words(lo, hi):
+            for tile, words in ((w8, words8), (w4, words4)):
+                view = tile[:].bitcast(I32).rearrange("p (e n) -> p e n", e=E)
+                nc.sync.dma_start(view[:, lo:hi], words.bitcast(I32)[:, lo:hi])
+
+        planes = weight_scales[:].bitcast(I32).rearrange("p (e n) -> p e n", e=E)
+        for quadrant in range(4):
             for scales, first_row in ((w8_scales, E4M3_ROW), (w4_scales, 0)):
                 start = 32 * quadrant + first_row
                 source = scales[:, 0, 4 * quadrant : 4 * quadrant + 4, :].rearrange("e q n -> q e n")
                 nc.sync.dma_start(planes[start : start + 4], source.bitcast(I32))
-
-        words8 = w8_words.rearrange("e a p n r -> p (e a) (n r)")
-        words4 = w4_words.rearrange("e a p n -> p (e a) n")
-        load_scales(0)
-        load_words(w8, words8, 0, 5)
-        load_words(w4, words4, 0, 5)
-        for quadrant in range(1, 4):
-            load_scales(quadrant)
+        load_words(E - 1, E)
         nc.sync.dma_start(bias[:], b)
-        load_words(w8, words8, 5, E)
-        load_words(w4, words4, 5, E)
-        for lo, hi in SCATTERS:
-            nc.sync.dma_start(gates[:, lo:hi], gate[:, lo:hi])
+        nc.sync.dma_start(gates[:, STARTS[E - 1] :], gate[:, STARTS[E - 1] :])
+        load_words(0, 5)
+        nc.sync.dma_start(gates[:, : STARTS[5]], gate[:, : STARTS[5]])
+        load_words(5, E - 1)
+        nc.sync.dma_start(gates[:, STARTS[5] : STARTS[E - 1]], gate[:, STARTS[5] : STARTS[E - 1]])
 
-        def rounding_views(g, lo, hi):
-            raw, t0 = [(tile, key[1]) for key, tile in raws.items() if key[0] == g and key[1] <= lo and hi <= key[2]][0]
+        def rounding_views(g, chunk, lo, hi):
             dst = rounded[g][:, lo * PACK : hi * PACK].rearrange("p (c i t) -> p c t i", i=2, t=PACK)
-            return dst, raw[:, :, lo - t0 : hi - t0].rearrange("p t (c i) -> p c t i", i=2)
+            return dst, raws[g, chunk][:, :, lo - chunk : hi - chunk].rearrange("p t (c i) -> p c t i", i=2)
+
+        def round_block(g, chunk, border, lo, hi):
+            if lo < border:
+                nc.vector.tensor_copy(*rounding_views(g, chunk, lo, min(hi, border)))
+            if border < hi:
+                nc.scalar.activation(*rounding_views(g, chunk, max(lo, border), hi), COPY)
 
         def quantize(g, lo, hi):
             nc.vector.quantize_mx(
@@ -148,54 +118,67 @@ def tile_moe_rag_lin_bias_kernel(
         def entries(lo, hi):
             return offsets[:, lo // GROUP : hi // GROUP]
 
-        def gather_words(g, lo, hi, tokens=T):
-            nc.vector.tensor_copy(slot_words[g][:, lo:hi], token_words[g][:, :tokens].indirect(entries(lo, hi)))
+        def gather_words(i, tokens):
+            lo, hi = PIECES[i]
+            tile = keep.tile([P, 384], U32, name=f"second_words{i}", tag="second_words", align_bytes=ALIGN)
+            nc.vector.tensor_copy(tile[:, : hi - lo], token_words[1][:, :tokens].indirect(entries(lo, hi)))
+            return tile
 
-        def gather_scales(lo, hi, tokens=T):
-            nc.vector.tensor_copy(late[0][:, lo:hi], token_scales[:, :tokens].indirect(entries(lo, hi)))
+        def gather_scales(i, tokens):
+            lo, hi = PIECES[i]
+            tag = f"raw1_{AHEAD[1]}" if i % 2 == 0 else "odd_scales"
+            tile = keep.tile([P, 384], U8, name=f"slot_scales{i}", tag=tag, align_bytes=ALIGN)
+            nc.vector.tensor_copy(tile[:, : hi - lo], token_scales[:, :tokens].indirect(entries(lo, hi)))
+            return tile
 
-        late = []
-        for kind, g, lo, hi, tokens in WORK:
-            if kind == "B":
-                late.append(keep.tile([P, T], U8, name="slot_scales", tag=f"raw1_{AHEAD[1]}", align_bytes=ALIGN))
-            if kind == "V":
-                nc.vector.tensor_copy(*rounding_views(g, lo, hi))
-            if kind == "S":
-                nc.scalar.activation(*rounding_views(g, lo, hi), COPY)
-            if kind == "Q":
-                quantize(g, lo, hi)
-            if kind == "W":
-                gather_words(g, lo, hi, tokens)
-            if kind == "B":
-                gather_scales(lo, hi, tokens)
+        def multiply(i, g, words, scales):
+            lo, hi = PIECES[i]
+            parts = [(e, c, min(c + WIDE, end)) for e, begin, end in runs(lo, hi) for c in range(begin, end, WIDE)]
+            for n, (e, c0, c1) in enumerate(parts):
+                columns = slice(e * N, (e + 1) * N)
+                if g == 0:
+                    nc.tensor.matmul_mx(
+                        out=banks[i][:, c0 - lo : c1 - lo],
+                        lhsT=w8[:, e * N * 4 : (e + 1) * N * 4].bitcast(FP8X4), lhsT_scale=weight_scales[E4M3_ROW:, columns],
+                        rhs=words[:, c0:c1].bitcast(FP8X4), rhs_scale=scales[E4M3_ROW:, c0 - lo : c1 - lo],
+                        start=n == 0, stop=False,
+                    )
+                else:
+                    nc.tensor.matmul_mx(
+                        out=banks[i][:, c0 - lo : c1 - lo],
+                        lhsT=w4[:, e * N * 2 : (e + 1) * N * 2].bitcast(FP4X4), lhsT_scale=weight_scales[:, columns],
+                        rhs=words[:, c0 - lo : c1 - lo].bitcast(FP8X4), rhs_scale=scales[:, c0 - lo : c1 - lo],
+                        start=False, stop=n == len(parts) - 1,
+                    )
 
-        for lo, hi in PIECES:
-            gather_words(1, lo, hi)
-            gather_scales(lo, hi)
-
-        slot_scales = late[0]
-        for e in range(E):
-            columns = slice(e * N, (e + 1) * N)
-            w8_e = w8[:, e * N * 4 : (e + 1) * N * 4].bitcast(FP8X4)
-            w4_e = w4[:, e * N * 2 : (e + 1) * N * 2].bitcast(FP4X4)
-            step = BANK if COUNTS[e] == BANK else 128
-            for c in range(0, COUNTS[e], step):
-                slots = slice(STARTS[e] + c, STARTS[e] + c + step)
-                acc = banks[e][:, c : c + step]
-                nc.tensor.matmul_mx(
-                    out=acc, lhsT=w8_e, lhsT_scale=weight_scales[E4M3_ROW:, columns],
-                    rhs=slot_words[0][:, slots].bitcast(FP8X4), rhs_scale=slot_scales[E4M3_ROW:, slots],
-                    start=True, stop=False,
+        def finish(i):
+            lo, hi = PIECES[i]
+            for e, begin, end in runs(lo, hi):
+                nc.vector.scalar_tensor_tensor(
+                    y[:, begin:end], banks[i][:, begin - lo : end - lo], bias[:, e : e + 1], gates[:, begin:end], ADD, MULT
                 )
-                nc.tensor.matmul_mx(
-                    out=acc, lhsT=w4_e, lhsT_scale=weight_scales[:, columns],
-                    rhs=slot_words[1][:, slots].bitcast(FP8X4), rhs_scale=slot_scales[:, slots],
-                    start=False, stop=True,
-                )
-            nc.scalar.activation(
-                y[:, STARTS[e] : STARTS[e + 1]], banks[e][:, : COUNTS[e]], IDENTITY, bias=bias[:, e : e + 1]
-            )
+            nc.scalar.activation(window[:].indirect(entries(lo, hi)), y[:, lo:hi], COPY)
 
-        for lo, hi in SCATTERS:
-            nc.vector.tensor_tensor(window[:].indirect(entries(lo, hi)), y[:, lo:hi], gates[:, lo:hi], MULT)
-        nc.sync.dma_start(out, window[:, :T])
+        for chunk, end, share in CHUNKS[0]:
+            for lo in range(chunk, end, BLOCK):
+                round_block(0, chunk, chunk + share, lo, min(lo + BLOCK, end))
+                quantize(0, lo, min(lo + BLOCK, end))
+        nc.vector.tensor_copy(first_words[:], token_words[0][:].indirect(offsets[:]))
+
+        for chunk, end, share in CHUNKS[1]:
+            round_block(1, chunk, chunk + share, chunk, end)
+            if end == T:
+                words = gather_words(0, AHEAD[1])
+            quantize(1, chunk, end)
+
+        scales = gather_scales(0, AHEAD[1])
+        multiply(0, 0, first_words, scales)
+        multiply(0, 1, words, scales)
+        for i in range(1, len(PIECES)):
+            scales = gather_scales(i, T)
+            multiply(i, 0, first_words, scales)
+            finish(i - 1)
+            words = gather_words(i, T)
+            multiply(i, 1, words, scales)
+        finish(len(PIECES) - 1)
+        nc.sync.dma_start(out, window[:])

@@ -35,7 +35,10 @@ CHUNKS = (
 )
 LAST_CHUNK = 256
 AHEAD = (STARTS[E - 1], T - LAST_CHUNK)
-PIECES = (AHEAD, (0, 384), (384, 768), (768, 1152), (1152, 1536), (AHEAD[1], T))
+PIECES = (AHEAD, (0, 256), (256, 640), (640, 1024), (1024, 1536), (AHEAD[1], T))
+ON_VECTOR = 4
+WINDOW = (1, 0, 1, 0, 0, 1)
+STORES = (0, 512, 1024, 1536, 1792, T)
 
 
 def runs(lo, hi):
@@ -55,17 +58,20 @@ def tile_moe_rag_lin_bias_kernel(
         w4 = keep.tile([P, E * N * 2], U8, name="w4", align_bytes=ALIGN)
         weight_scales = keep.tile([P, E * N], U8, name="weight_scales", align_bytes=ALIGN)
         bias = keep.tile([P, E], F32, name="bias")
-        gates = keep.tile([P, T], F32, name="gates", align_bytes=ALIGN)
+        gates = [keep.tile([P, hi - lo], F32, name=f"gates{i}", tag=f"gates{i}", align_bytes=ALIGN) for i, (lo, hi) in enumerate(PIECES)]
         token_scales = keep.tile([P, T], U8, name="token_scales", align_bytes=ALIGN)
         token_words = [keep.tile([P, (2 - g) * T], U32, name=f"token_words{g}", align_bytes=ALIGN) for g in range(2)]
         first_words = keep.tile([P, T], U32, name="first_words", align_bytes=ALIGN)
         rounded = [keep.tile([P, T * PACK], BF16, name=f"rounded{g}", align_bytes=ALIGN) for g in range(2)]
         y = keep.tile([P, T], F32, name="y", align_bytes=ALIGN)
-        window = keep.tile([P, T], F32, name="window", align_bytes=ALIGN)
+        windows = [keep.tile([P, T], F32, name=f"window{w}", align_bytes=ALIGN) for w in range(2)]
+        result = keep.tile([P, T], F32, name="result", align_bytes=ALIGN)
         banks = [psum.tile([P, BANK], F32, name=f"bank{i}") for i in range(len(PIECES))]
 
         nc.vector.memset(weight_scales[:].bitcast(I32), 0)
         nc.vector.memset(token_scales[:].bitcast(I32), 0)
+        for window in windows:
+            nc.vector.memset(window[:], 0.0)
 
         raws = {}
         for g in range(2):
@@ -90,13 +96,19 @@ def tile_moe_rag_lin_bias_kernel(
                 start = 32 * quadrant + first_row
                 source = scales[:, 0, 4 * quadrant : 4 * quadrant + 4, :].rearrange("e q n -> q e n")
                 nc.sync.dma_start(planes[start : start + 4], source.bitcast(I32))
+
+        def load_gates(i):
+            nc.sync.dma_start(gates[i][:], gate[:, PIECES[i][0] : PIECES[i][1]])
+
         load_words(E - 1, E)
         nc.sync.dma_start(bias[:], b)
-        nc.sync.dma_start(gates[:, STARTS[E - 1] :], gate[:, STARTS[E - 1] :])
-        load_words(0, 5)
-        nc.sync.dma_start(gates[:, : STARTS[5]], gate[:, : STARTS[5]])
-        load_words(5, E - 1)
-        nc.sync.dma_start(gates[:, STARTS[5] : STARTS[E - 1]], gate[:, STARTS[5] : STARTS[E - 1]])
+        load_gates(0)
+        load_words(0, 4)
+        load_gates(1)
+        load_gates(2)
+        load_words(4, E - 1)
+        for i in range(3, len(PIECES)):
+            load_gates(i)
 
         def rounding_views(g, chunk, lo, hi):
             dst = rounded[g][:, lo * PACK : hi * PACK].rearrange("p (c i t) -> p c t i", i=2, t=PACK)
@@ -120,14 +132,14 @@ def tile_moe_rag_lin_bias_kernel(
 
         def gather_words(i, tokens):
             lo, hi = PIECES[i]
-            tile = keep.tile([P, 384], U32, name=f"second_words{i}", tag="second_words", align_bytes=ALIGN)
+            tile = keep.tile([P, hi - lo], U32, name=f"second_words{i}", tag=f"second_words{min(i, 1)}", align_bytes=ALIGN)
             nc.vector.tensor_copy(tile[:, : hi - lo], token_words[1][:, :tokens].indirect(entries(lo, hi)))
             return tile
 
         def gather_scales(i, tokens):
             lo, hi = PIECES[i]
-            tag = f"raw1_{AHEAD[1]}" if i % 2 == 0 else "odd_scales"
-            tile = keep.tile([P, 384], U8, name=f"slot_scales{i}", tag=tag, align_bytes=ALIGN)
+            tag = (f"raw1_{AHEAD[1]}", "slot_scales1")[i] if i < 2 else f"gates{i - 2}"
+            tile = keep.tile([P, hi - lo], U8, name=f"slot_scales{i}", tag=tag, align_bytes=ALIGN)
             nc.vector.tensor_copy(tile[:, : hi - lo], token_scales[:, :tokens].indirect(entries(lo, hi)))
             return tile
 
@@ -155,9 +167,16 @@ def tile_moe_rag_lin_bias_kernel(
             lo, hi = PIECES[i]
             for e, begin, end in runs(lo, hi):
                 nc.vector.scalar_tensor_tensor(
-                    y[:, begin:end], banks[i][:, begin - lo : end - lo], bias[:, e : e + 1], gates[:, begin:end], ADD, MULT
+                    y[:, begin:end], banks[i][:, begin - lo : end - lo], bias[:, e : e + 1], gates[i][:, begin - lo : end - lo], ADD, MULT
                 )
-            nc.scalar.activation(window[:].indirect(entries(lo, hi)), y[:, lo:hi], COPY)
+
+        def scatter(i):
+            lo, hi = PIECES[i]
+            target = windows[WINDOW[i]][:].indirect(entries(lo, hi))
+            if i == ON_VECTOR:
+                nc.vector.tensor_copy(target, y[:, lo:hi])
+            else:
+                nc.scalar.activation(target, y[:, lo:hi], COPY)
 
         for chunk, end, share in CHUNKS[0]:
             for lo in range(chunk, end, BLOCK):
@@ -177,8 +196,14 @@ def tile_moe_rag_lin_bias_kernel(
         for i in range(1, len(PIECES)):
             scales = gather_scales(i, T)
             multiply(i, 0, first_words, scales)
-            finish(i - 1)
             words = gather_words(i, T)
             multiply(i, 1, words, scales)
+            finish(i - 1)
+            if i - 1 != ON_VECTOR:
+                scatter(i - 1)
         finish(len(PIECES) - 1)
-        nc.sync.dma_start(out, window[:])
+        scatter(len(PIECES) - 1)
+        scatter(ON_VECTOR)
+        for lo, hi in zip(STORES, STORES[1:]):
+            nc.vector.tensor_tensor(result[:, lo:hi], windows[0][:, lo:hi], windows[1][:, lo:hi], ADD)
+            nc.sync.dma_start(out[:, lo:hi], result[:, lo:hi])

@@ -35,14 +35,11 @@ CHUNKS = (
 )
 LAST_CHUNK = 256
 AHEAD = (STARTS[E - 1], T - LAST_CHUNK)
-PIECES = (AHEAD, (0, 256), (256, 640), (640, 1024), (1024, 1536), (AHEAD[1], T))
-ON_VECTOR = 4
-WINDOW = (1, 0, 1, 0, 0, 1)
+FIRST = STARTS[5]
+PIECES = ((0, FIRST), (FIRST, AHEAD[0]), (AHEAD[1], T))
+ON_SCALAR = ((0, 384), (384, 768), (768, 1152))
+GATE_TILES = ((0, 256), (256, 384), (384, 640), (640, 768), (768, T))
 STORES = (0, 512, 1024, 1536, 1792, T)
-
-
-def runs(lo, hi):
-    return [(e, max(lo, STARTS[e]), min(hi, STARTS[e + 1])) for e in range(E) if STARTS[e] < hi and lo < STARTS[e + 1]]
 
 
 def tile_moe_rag_lin_bias_kernel(
@@ -58,7 +55,7 @@ def tile_moe_rag_lin_bias_kernel(
         w4 = keep.tile([P, E * N * 2], U8, name="w4", align_bytes=ALIGN)
         weight_scales = keep.tile([P, E * N], U8, name="weight_scales", align_bytes=ALIGN)
         bias = keep.tile([P, E], F32, name="bias")
-        gates = [keep.tile([P, hi - lo], F32, name=f"gates{i}", tag=f"gates{i}", align_bytes=ALIGN) for i, (lo, hi) in enumerate(PIECES)]
+        gates = {lo: keep.tile([P, hi - lo], F32, name=f"gates{lo}", tag=f"gates{lo}", align_bytes=ALIGN) for lo, hi in GATE_TILES}
         token_scales = keep.tile([P, T], U8, name="token_scales", align_bytes=ALIGN)
         token_words = [keep.tile([P, (2 - g) * T], U32, name=f"token_words{g}", align_bytes=ALIGN) for g in range(2)]
         first_words = keep.tile([P, T], U32, name="first_words", align_bytes=ALIGN)
@@ -66,7 +63,7 @@ def tile_moe_rag_lin_bias_kernel(
         y = keep.tile([P, T], F32, name="y", align_bytes=ALIGN)
         windows = [keep.tile([P, T], F32, name=f"window{w}", align_bytes=ALIGN) for w in range(2)]
         result = keep.tile([P, T], F32, name="result", align_bytes=ALIGN)
-        banks = [psum.tile([P, BANK], F32, name=f"bank{i}") for i in range(len(PIECES))]
+        banks = [psum.tile([P, BANK], F32, name=f"bank{i}") for i in range(E)]
 
         nc.vector.memset(weight_scales[:].bitcast(I32), 0)
         nc.vector.memset(token_scales[:].bitcast(I32), 0)
@@ -97,18 +94,13 @@ def tile_moe_rag_lin_bias_kernel(
                 source = scales[:, 0, 4 * quadrant : 4 * quadrant + 4, :].rearrange("e q n -> q e n")
                 nc.sync.dma_start(planes[start : start + 4], source.bitcast(I32))
 
-        def load_gates(i):
-            nc.sync.dma_start(gates[i][:], gate[:, PIECES[i][0] : PIECES[i][1]])
-
-        load_words(E - 1, E)
+        load_words(0, 5)
         nc.sync.dma_start(bias[:], b)
-        load_gates(0)
-        load_words(0, 4)
-        load_gates(1)
-        load_gates(2)
-        load_words(4, E - 1)
-        for i in range(3, len(PIECES)):
-            load_gates(i)
+        for lo, hi in GATE_TILES[:4]:
+            nc.sync.dma_start(gates[lo][:], gate[:, lo:hi])
+        load_words(5, E)
+        for lo, hi in GATE_TILES[4:]:
+            nc.sync.dma_start(gates[lo][:], gate[:, lo:hi])
 
         def rounding_views(g, chunk, lo, hi):
             dst = rounded[g][:, lo * PACK : hi * PACK].rearrange("p (c i t) -> p c t i", i=2, t=PACK)
@@ -130,53 +122,43 @@ def tile_moe_rag_lin_bias_kernel(
         def entries(lo, hi):
             return offsets[:, lo // GROUP : hi // GROUP]
 
-        def gather_words(i, tokens):
-            lo, hi = PIECES[i]
-            tile = keep.tile([P, hi - lo], U32, name=f"second_words{i}", tag=f"second_words{min(i, 1)}", align_bytes=ALIGN)
-            nc.vector.tensor_copy(tile[:, : hi - lo], token_words[1][:, :tokens].indirect(entries(lo, hi)))
-            return tile
+        second_words = {}
+        slot_scales = {}
 
-        def gather_scales(i, tokens):
-            lo, hi = PIECES[i]
-            tag = (f"raw1_{AHEAD[1]}", "slot_scales1")[i] if i < 2 else f"gates{i - 2}"
-            tile = keep.tile([P, hi - lo], U8, name=f"slot_scales{i}", tag=tag, align_bytes=ALIGN)
-            nc.vector.tensor_copy(tile[:, : hi - lo], token_scales[:, :tokens].indirect(entries(lo, hi)))
-            return tile
+        def gather_words(lo, hi, tokens, tag):
+            second_words[lo] = keep.tile([P, hi - lo], U32, name=f"second_words{lo}", tag=tag, align_bytes=ALIGN)
+            nc.vector.tensor_copy(second_words[lo][:], token_words[1][:, :tokens].indirect(entries(lo, hi)))
 
-        def multiply(i, g, words, scales):
-            lo, hi = PIECES[i]
-            parts = [(e, c, min(c + WIDE, end)) for e, begin, end in runs(lo, hi) for c in range(begin, end, WIDE)]
-            for n, (e, c0, c1) in enumerate(parts):
-                columns = slice(e * N, (e + 1) * N)
+        def gather_scales(lo, hi, tokens, tag):
+            slot_scales[lo] = keep.tile([P, hi - lo], U8, name=f"slot_scales{lo}", tag=tag, align_bytes=ALIGN)
+            nc.vector.tensor_copy(slot_scales[lo][:], token_scales[:, :tokens].indirect(entries(lo, hi)))
+
+        def multiply(e, g):
+            columns = slice(e * N, (e + 1) * N)
+            for c0 in range(STARTS[e], STARTS[e + 1], WIDE):
+                c1 = min(c0 + WIDE, STARTS[e + 1])
+                base = max(lo for lo in slot_scales if lo <= c0)
+                scales = slot_scales[base]
+                acc = banks[e][:, c0 - STARTS[e] : c1 - STARTS[e]]
                 if g == 0:
                     nc.tensor.matmul_mx(
-                        out=banks[i][:, c0 - lo : c1 - lo],
-                        lhsT=w8[:, e * N * 4 : (e + 1) * N * 4].bitcast(FP8X4), lhsT_scale=weight_scales[E4M3_ROW:, columns],
-                        rhs=words[:, c0:c1].bitcast(FP8X4), rhs_scale=scales[E4M3_ROW:, c0 - lo : c1 - lo],
-                        start=n == 0, stop=False,
+                        out=acc, lhsT=w8[:, e * N * 4 : (e + 1) * N * 4].bitcast(FP8X4), lhsT_scale=weight_scales[E4M3_ROW:, columns],
+                        rhs=first_words[:, c0:c1].bitcast(FP8X4), rhs_scale=scales[E4M3_ROW:, c0 - base : c1 - base],
+                        start=c0 == STARTS[e], stop=False,
                     )
                 else:
                     nc.tensor.matmul_mx(
-                        out=banks[i][:, c0 - lo : c1 - lo],
-                        lhsT=w4[:, e * N * 2 : (e + 1) * N * 2].bitcast(FP4X4), lhsT_scale=weight_scales[:, columns],
-                        rhs=words[:, c0 - lo : c1 - lo].bitcast(FP8X4), rhs_scale=scales[:, c0 - lo : c1 - lo],
-                        start=False, stop=n == len(parts) - 1,
+                        out=acc, lhsT=w4[:, e * N * 2 : (e + 1) * N * 2].bitcast(FP4X4), lhsT_scale=weight_scales[:, columns],
+                        rhs=second_words[base][:, c0 - base : c1 - base].bitcast(FP8X4), rhs_scale=scales[:, c0 - base : c1 - base],
+                        start=False, stop=c1 == STARTS[e + 1],
                     )
 
-        def finish(i):
-            lo, hi = PIECES[i]
-            for e, begin, end in runs(lo, hi):
-                nc.vector.scalar_tensor_tensor(
-                    y[:, begin:end], banks[i][:, begin - lo : end - lo], bias[:, e : e + 1], gates[i][:, begin - lo : end - lo], ADD, MULT
-                )
-
-        def scatter(i):
-            lo, hi = PIECES[i]
-            target = windows[WINDOW[i]][:].indirect(entries(lo, hi))
-            if i == ON_VECTOR:
-                nc.vector.tensor_copy(target, y[:, lo:hi])
-            else:
-                nc.scalar.activation(target, y[:, lo:hi], COPY)
+        def finish(e):
+            begin, end = STARTS[e], STARTS[e + 1]
+            base = max(lo for lo in gates if lo <= begin)
+            nc.vector.scalar_tensor_tensor(
+                y[:, begin:end], banks[e][:, : end - begin], bias[:, e : e + 1], gates[base][:, begin - base : end - base], ADD, MULT
+            )
 
         for chunk, end, share in CHUNKS[0]:
             for lo in range(chunk, end, BLOCK):
@@ -187,23 +169,31 @@ def tile_moe_rag_lin_bias_kernel(
         for chunk, end, share in CHUNKS[1]:
             round_block(1, chunk, chunk + share, chunk, end)
             if end == T:
-                words = gather_words(0, AHEAD[1])
+                gather_words(*AHEAD, AHEAD[1], "ahead_words")
             quantize(1, chunk, end)
 
-        scales = gather_scales(0, AHEAD[1])
-        multiply(0, 0, first_words, scales)
-        multiply(0, 1, words, scales)
-        for i in range(1, len(PIECES)):
-            scales = gather_scales(i, T)
-            multiply(i, 0, first_words, scales)
-            words = gather_words(i, T)
-            multiply(i, 1, words, scales)
-            finish(i - 1)
-            if i - 1 != ON_VECTOR:
-                scatter(i - 1)
-        finish(len(PIECES) - 1)
-        scatter(len(PIECES) - 1)
-        scatter(ON_VECTOR)
+        gather_scales(*AHEAD, AHEAD[1], f"raw1_{AHEAD[1]}")
+        gather_scales(*PIECES[0], T, "early_scales")
+        gather_words(*PIECES[0], T, "early_words")
+        gather_scales(*PIECES[2], T, "last_scales")
+        gather_words(*PIECES[2], T, "last_words")
+        for g in range(2):
+            for e in range(5):
+                multiply(e, g)
+        for g in range(2):
+            multiply(E - 1, g)
+        for e in range(5):
+            finish(e)
+        gather_scales(*PIECES[1], T, "gates256")
+        gather_words(*PIECES[1], T, "gates640")
+        for g in range(2):
+            for e in (5, 6):
+                multiply(e, g)
+        for e in (7, 5, 6):
+            finish(e)
+        for lo, hi in ON_SCALAR:
+            nc.scalar.activation(windows[1][:].indirect(entries(lo, hi)), y[:, lo:hi], COPY)
+        nc.vector.tensor_copy(windows[0][:].indirect(entries(STARTS[6], T)), y[:, STARTS[6] :])
         for lo, hi in zip(STORES, STORES[1:]):
             nc.vector.tensor_tensor(result[:, lo:hi], windows[0][:, lo:hi], windows[1][:, lo:hi], ADD)
             nc.sync.dma_start(out[:, lo:hi], result[:, lo:hi])

@@ -26,6 +26,7 @@ U8 = mybir.dt.uint8
 FP8X4 = mybir.dt.float8_e4m3fn_x4
 FP4X4 = mybir.dt.float4_e2m1fn_x4
 COPY = mybir.ActivationFunctionType.Copy
+IDENTITY = mybir.ActivationFunctionType.Identity
 ADD = mybir.AluOpType.add
 MULT = mybir.AluOpType.mult
 
@@ -35,10 +36,9 @@ CHUNKS = (
 )
 LAST_CHUNK = 256
 AHEAD = (STARTS[E - 1], T - LAST_CHUNK)
-FIRST = STARTS[5]
-PIECES = ((0, FIRST), (FIRST, AHEAD[0]), (AHEAD[1], T))
-ON_SCALAR = ((0, 384), (384, 768), (768, 1152))
-GATE_TILES = ((0, 256), (256, 384), (384, 640), (640, 768), (768, T))
+SPLIT = 960
+PIECES = ((STARTS[5], STARTS[7]), (AHEAD[1], T), (STARTS[3], STARTS[5]), (0, STARTS[3]))
+ON_SCALAR = ((640, 960), (320, 640), (0, 320))
 STORES = (0, 512, 1024, 1536, 1792, T)
 
 
@@ -55,20 +55,20 @@ def tile_moe_rag_lin_bias_kernel(
         w4 = keep.tile([P, E * N * 2], U8, name="w4", align_bytes=ALIGN)
         weight_scales = keep.tile([P, E * N], U8, name="weight_scales", align_bytes=ALIGN)
         bias = keep.tile([P, E], F32, name="bias")
-        gates = {lo: keep.tile([P, hi - lo], F32, name=f"gates{lo}", tag=f"gates{lo}", align_bytes=ALIGN) for lo, hi in GATE_TILES}
+        gates = keep.tile([P, T], F32, name="gates", align_bytes=ALIGN)
         token_scales = keep.tile([P, T], U8, name="token_scales", align_bytes=ALIGN)
         token_words = [keep.tile([P, (2 - g) * T], U32, name=f"token_words{g}", align_bytes=ALIGN) for g in range(2)]
         first_words = keep.tile([P, T], U32, name="first_words", align_bytes=ALIGN)
         rounded = [keep.tile([P, T * PACK], BF16, name=f"rounded{g}", align_bytes=ALIGN) for g in range(2)]
         y = keep.tile([P, T], F32, name="y", align_bytes=ALIGN)
-        windows = [keep.tile([P, T], F32, name=f"window{w}", align_bytes=ALIGN) for w in range(2)]
+        windows = [keep.tile([P, (2 - w) * T], F32, name=f"window{w}", align_bytes=ALIGN) for w in range(2)]
         result = keep.tile([P, T], F32, name="result", align_bytes=ALIGN)
         banks = [psum.tile([P, BANK], F32, name=f"bank{i}") for i in range(E)]
 
         nc.vector.memset(weight_scales[:].bitcast(I32), 0)
         nc.vector.memset(token_scales[:].bitcast(I32), 0)
         for window in windows:
-            nc.vector.memset(window[:], 0.0)
+            nc.vector.memset(window[:, :T], 0.0)
 
         raws = {}
         for g in range(2):
@@ -94,13 +94,11 @@ def tile_moe_rag_lin_bias_kernel(
                 source = scales[:, 0, 4 * quadrant : 4 * quadrant + 4, :].rearrange("e q n -> q e n")
                 nc.sync.dma_start(planes[start : start + 4], source.bitcast(I32))
 
-        load_words(0, 5)
-        nc.sync.dma_start(bias[:], b)
-        for lo, hi in GATE_TILES[:4]:
-            nc.sync.dma_start(gates[lo][:], gate[:, lo:hi])
         load_words(5, E)
-        for lo, hi in GATE_TILES[4:]:
-            nc.sync.dma_start(gates[lo][:], gate[:, lo:hi])
+        nc.sync.dma_start(bias[:], b)
+        load_words(0, 5)
+        nc.sync.dma_start(gates[:, :SPLIT], gate[:, :SPLIT])
+        nc.sync.dma_start(gates[:, SPLIT:], gate[:, SPLIT:])
 
         def rounding_views(g, chunk, lo, hi):
             dst = rounded[g][:, lo * PACK : hi * PACK].rearrange("p (c i t) -> p c t i", i=2, t=PACK)
@@ -153,11 +151,16 @@ def tile_moe_rag_lin_bias_kernel(
                         start=False, stop=c1 == STARTS[e + 1],
                     )
 
-        def finish(e):
-            begin, end = STARTS[e], STARTS[e + 1]
-            base = max(lo for lo in gates if lo <= begin)
+        def bias_and_gate(e):
+            begin, end = STARTS[e], min(STARTS[e + 1], SPLIT)
             nc.vector.scalar_tensor_tensor(
-                y[:, begin:end], banks[e][:, : end - begin], bias[:, e : e + 1], gates[base][:, begin - base : end - base], ADD, MULT
+                y[:, begin:end], banks[e][:, : end - begin], bias[:, e : e + 1], gates[:, begin:end], ADD, MULT
+            )
+
+        def bias_alone(e):
+            begin, end = max(STARTS[e], SPLIT), STARTS[e + 1]
+            nc.scalar.activation(
+                y[:, begin:end], banks[e][:, begin - STARTS[e] : end - STARTS[e]], IDENTITY, bias=bias[:, e : e + 1]
             )
 
         for chunk, end, share in CHUNKS[0]:
@@ -173,27 +176,20 @@ def tile_moe_rag_lin_bias_kernel(
             quantize(1, chunk, end)
 
         gather_scales(*AHEAD, AHEAD[1], f"raw1_{AHEAD[1]}")
-        gather_scales(*PIECES[0], T, "early_scales")
-        gather_words(*PIECES[0], T, "early_words")
-        gather_scales(*PIECES[2], T, "last_scales")
-        gather_words(*PIECES[2], T, "last_words")
-        for g in range(2):
-            for e in range(5):
-                multiply(e, g)
-        for g in range(2):
-            multiply(E - 1, g)
-        for e in range(5):
-            finish(e)
-        gather_scales(*PIECES[1], T, "gates256")
-        gather_words(*PIECES[1], T, "gates640")
-        for g in range(2):
-            for e in (5, 6):
-                multiply(e, g)
-        for e in (7, 5, 6):
-            finish(e)
+        for lo, hi in PIECES:
+            gather_scales(lo, hi, T, f"scales{lo}")
+            gather_words(lo, hi, T, f"words{lo}")
+            for g in range(2):
+                for e in range(E):
+                    if lo < STARTS[e + 1] <= hi:
+                        multiply(e, g)
+        for e in (5, 6, 7):
+            bias_alone(e)
+        for e in (5, 4, 3, 2, 1, 0):
+            bias_and_gate(e)
         for lo, hi in ON_SCALAR:
             nc.scalar.activation(windows[1][:].indirect(entries(lo, hi)), y[:, lo:hi], COPY)
-        nc.vector.tensor_copy(windows[0][:].indirect(entries(STARTS[6], T)), y[:, STARTS[6] :])
+        nc.vector.tensor_tensor(windows[0][:].indirect(entries(SPLIT, T)), y[:, SPLIT:], gates[:, SPLIT:], MULT)
         for lo, hi in zip(STORES, STORES[1:]):
             nc.vector.tensor_tensor(result[:, lo:hi], windows[0][:, lo:hi], windows[1][:, lo:hi], ADD)
             nc.sync.dma_start(out[:, lo:hi], result[:, lo:hi])

@@ -12,6 +12,7 @@ PACK = 4
 K_PASS = P * PACK
 BANK = 512
 GROUP = 16
+QUADRANT = 32
 ALIGN = 256
 E4M3_ROW = 4
 BLOCK = 512
@@ -37,9 +38,14 @@ CHUNKS = (
 LAST_CHUNK = 256
 AHEAD = (STARTS[E - 1], T - LAST_CHUNK)
 SPLIT = 960
-PIECES = ((STARTS[5], STARTS[7]), (AHEAD[1], T), (STARTS[3], STARTS[5]), (0, STARTS[3]))
-ON_SCALAR = ((640, 960), (320, 640), (0, 320))
-STORES = (0, 512, 1024, 1536, 1792, T)
+SHARED = 5
+PIECES = ((STARTS[SHARED], STARTS[7]), (AHEAD[1], T), (STARTS[3], STARTS[SHARED]), (0, STARTS[3]))
+ON_SCALAR = (
+    (STARTS[3], STARTS[4], (3,)),
+    (STARTS[4], SPLIT, (SHARED, 4)),
+    (0, STARTS[3], (2, 1, 0)),
+)
+STORES = (0, 256, 640, 1152, 1664, T)
 
 
 def tile_moe_rag_lin_bias_kernel(
@@ -83,20 +89,20 @@ def tile_moe_rag_lin_bias_kernel(
         words4 = w4_words.rearrange("e a p n -> p (e a) n")
 
         def load_words(lo, hi):
-            for tile, words in ((w8, words8), (w4, words4)):
+            for tile, words in ((w4, words4), (w8, words8)):
                 view = tile[:].bitcast(I32).rearrange("p (e n) -> p e n", e=E)
                 nc.sync.dma_start(view[:, lo:hi], words.bitcast(I32)[:, lo:hi])
 
         planes = weight_scales[:].bitcast(I32).rearrange("p (e n) -> p e n", e=E)
-        for quadrant in range(4):
+        for quadrant in range(P // QUADRANT):
             for scales, first_row in ((w8_scales, E4M3_ROW), (w4_scales, 0)):
-                start = 32 * quadrant + first_row
+                start = QUADRANT * quadrant + first_row
                 source = scales[:, 0, 4 * quadrant : 4 * quadrant + 4, :].rearrange("e q n -> q e n")
                 nc.sync.dma_start(planes[start : start + 4], source.bitcast(I32))
 
-        load_words(5, E)
+        load_words(SHARED, E)
         nc.sync.dma_start(bias[:], b)
-        load_words(0, 5)
+        load_words(0, SHARED)
         nc.sync.dma_start(gates[:, :SPLIT], gate[:, :SPLIT])
         nc.sync.dma_start(gates[:, SPLIT:], gate[:, SPLIT:])
 
@@ -180,14 +186,15 @@ def tile_moe_rag_lin_bias_kernel(
             gather_scales(lo, hi, T, f"scales{lo}")
             gather_words(lo, hi, T, f"words{lo}")
             for g in range(2):
-                for e in range(E):
+                for e in reversed(range(E)):
                     if lo < STARTS[e + 1] <= hi:
                         multiply(e, g)
-        for e in (5, 6, 7):
+        for e in range(SHARED, E):
             bias_alone(e)
-        for e in (5, 4, 3, 2, 1, 0):
-            bias_and_gate(e)
-        for lo, hi in ON_SCALAR:
+        for lo, hi, experts in ON_SCALAR:
+            for e in experts:
+                bias_and_gate(e)
+        for lo, hi, experts in ON_SCALAR:
             nc.scalar.activation(windows[1][:].indirect(entries(lo, hi)), y[:, lo:hi], COPY)
         nc.vector.tensor_tensor(windows[0][:].indirect(entries(SPLIT, T)), y[:, SPLIT:], gates[:, SPLIT:], MULT)
         for lo, hi in zip(STORES, STORES[1:]):

@@ -37,14 +37,19 @@ CHUNKS = (
 )
 LAST_CHUNK = 256
 AHEAD = (STARTS[E - 1], T - LAST_CHUNK)
-SPLIT = 960
-SHARED = 5
-PIECES = ((STARTS[SHARED], STARTS[7]), (AHEAD[1], T), (STARTS[3], STARTS[SHARED]), (0, STARTS[3]))
-ON_SCALAR = (
-    (STARTS[3], STARTS[4], (3,)),
-    (STARTS[4], SPLIT, (SHARED, 4)),
-    (0, STARTS[3], (2, 1, 0)),
-)
+OWN = (1024, STARTS[7])
+RUNS = {
+    "0": (0, STARTS[0], STARTS[1], 0, 0),
+    "1": (1, STARTS[1], STARTS[2], 1, 0),
+    "2": (2, STARTS[2], STARTS[3], 2, 0),
+    "3": (3, STARTS[3], STARTS[4], 3, 0),
+    "4": (4, STARTS[4], STARTS[5], 3, COUNTS[3]),
+    "5a": (5, STARTS[5], OWN[0], 4, 0),
+    "5b": (5, OWN[0], STARTS[6], 5, 0),
+    "6": (6, STARTS[6], STARTS[7], 5, STARTS[6] - OWN[0]),
+    "7a": (7, STARTS[7], AHEAD[1], 6, 0),
+    "7b": (7, AHEAD[1], T, 7, 0),
+}
 STORES = (0, 256, 640, 1152, 1664, T)
 
 
@@ -54,6 +59,7 @@ def tile_moe_rag_lin_bias_kernel(
     nc = tc.nc
     with ExitStack() as ctx:
         keep = ctx.enter_context(tc.tile_pool(name="keep", bufs=1))
+        turns = ctx.enter_context(tc.tile_pool(name="turns", bufs=1))
         psum = ctx.enter_context(tc.psum_pool(name="psum", bufs=1))
 
         offsets = keep.tile([P, T // GROUP], U16, name="offsets")
@@ -61,7 +67,6 @@ def tile_moe_rag_lin_bias_kernel(
         w4 = keep.tile([P, E * N * 2], U8, name="w4", align_bytes=ALIGN)
         weight_scales = keep.tile([P, E * N], U8, name="weight_scales", align_bytes=ALIGN)
         bias = keep.tile([P, E], F32, name="bias")
-        gates = keep.tile([P, T], F32, name="gates", align_bytes=ALIGN)
         token_scales = keep.tile([P, T], U8, name="token_scales", align_bytes=ALIGN)
         token_words = [keep.tile([P, (2 - g) * T], U32, name=f"token_words{g}", align_bytes=ALIGN) for g in range(2)]
         first_words = keep.tile([P, T], U32, name="first_words", align_bytes=ALIGN)
@@ -100,11 +105,28 @@ def tile_moe_rag_lin_bias_kernel(
                 source = scales[:, 0, 4 * quadrant : 4 * quadrant + 4, :].rearrange("e q n -> q e n")
                 nc.sync.dma_start(planes[start : start + 4], source.bitcast(I32))
 
-        load_words(SHARED, E)
+        gates = {}
+
+        def load_gates(lo, hi, offset=None):
+            if offset is None:
+                gates[lo] = keep.tile([P, hi - lo], F32, name=f"gates{lo}", align_bytes=ALIGN)
+            else:
+                gates[lo] = turns.tile([P, hi - lo], F32, name=f"gates{lo}", offset=offset, align_bytes=ALIGN)
+            nc.sync.dma_start(gates[lo][:], gate[:, lo:hi])
+
+        def gate_columns(lo, hi):
+            base = max(first for first in gates if first <= lo)
+            return gates[base][:, lo - base : hi - base]
+
+        load_words(7, E)
+        load_words(0, 5)
         nc.sync.dma_start(bias[:], b)
-        load_words(0, SHARED)
-        nc.sync.dma_start(gates[:, :SPLIT], gate[:, :SPLIT])
-        nc.sync.dma_start(gates[:, SPLIT:], gate[:, SPLIT:])
+        load_gates(*AHEAD, offset=0)
+        load_gates(0, STARTS[3])
+        load_gates(STARTS[3], STARTS[4], offset=6912)
+        load_words(5, 7)
+        load_gates(STARTS[4], STARTS[7])
+        load_gates(AHEAD[1], T)
 
         def rounding_views(g, chunk, lo, hi):
             dst = rounded[g][:, lo * PACK : hi * PACK].rearrange("p (c i t) -> p c t i", i=2, t=PACK)
@@ -129,45 +151,61 @@ def tile_moe_rag_lin_bias_kernel(
         second_words = {}
         slot_scales = {}
 
-        def gather_words(lo, hi, tokens, tag):
-            second_words[lo] = keep.tile([P, hi - lo], U32, name=f"second_words{lo}", tag=tag, align_bytes=ALIGN)
+        def gathered(lo, hi, dtype, name, place):
+            if isinstance(place, str):
+                return keep.tile([P, hi - lo], dtype, name=name, tag=place, align_bytes=ALIGN)
+            return turns.tile([P, hi - lo], dtype, name=name, offset=place, align_bytes=ALIGN)
+
+        def gather_words(lo, hi, tokens, place):
+            second_words[lo] = gathered(lo, hi, U32, f"second_words{lo}", place)
             nc.vector.tensor_copy(second_words[lo][:], token_words[1][:, :tokens].indirect(entries(lo, hi)))
 
-        def gather_scales(lo, hi, tokens, tag):
-            slot_scales[lo] = keep.tile([P, hi - lo], U8, name=f"slot_scales{lo}", tag=tag, align_bytes=ALIGN)
+        def gather_scales(lo, hi, tokens, place):
+            slot_scales[lo] = gathered(lo, hi, U8, f"slot_scales{lo}", place)
             nc.vector.tensor_copy(slot_scales[lo][:], token_scales[:, :tokens].indirect(entries(lo, hi)))
 
-        def multiply(e, g):
+        def multiply(run, g, opens, closes):
+            e, begin, end, bank, column = RUNS[run]
             columns = slice(e * N, (e + 1) * N)
-            for c0 in range(STARTS[e], STARTS[e + 1], WIDE):
-                c1 = min(c0 + WIDE, STARTS[e + 1])
+            for c0 in range(begin, end, WIDE):
+                c1 = min(c0 + WIDE, end)
                 base = max(lo for lo in slot_scales if lo <= c0)
                 scales = slot_scales[base]
-                acc = banks[e][:, c0 - STARTS[e] : c1 - STARTS[e]]
+                acc = banks[bank][:, column + c0 - begin : column + c1 - begin]
                 if g == 0:
                     nc.tensor.matmul_mx(
                         out=acc, lhsT=w8[:, e * N * 4 : (e + 1) * N * 4].bitcast(FP8X4), lhsT_scale=weight_scales[E4M3_ROW:, columns],
                         rhs=first_words[:, c0:c1].bitcast(FP8X4), rhs_scale=scales[E4M3_ROW:, c0 - base : c1 - base],
-                        start=c0 == STARTS[e], stop=False,
+                        start=opens and c0 == begin, stop=False,
                     )
                 else:
+                    first = max(lo for lo in second_words if lo <= c0)
                     nc.tensor.matmul_mx(
                         out=acc, lhsT=w4[:, e * N * 2 : (e + 1) * N * 2].bitcast(FP4X4), lhsT_scale=weight_scales[:, columns],
-                        rhs=second_words[base][:, c0 - base : c1 - base].bitcast(FP8X4), rhs_scale=scales[:, c0 - base : c1 - base],
-                        start=False, stop=c1 == STARTS[e + 1],
+                        rhs=second_words[first][:, c0 - first : c1 - first].bitcast(FP8X4), rhs_scale=scales[:, c0 - base : c1 - base],
+                        start=False, stop=closes and c1 == end,
                     )
 
-        def bias_and_gate(e):
-            begin, end = STARTS[e], min(STARTS[e + 1], SPLIT)
+        def products(g, *runs):
+            for run in runs:
+                mates = [r for r in runs if RUNS[r][3] == RUNS[run][3]]
+                multiply(run, g, run == mates[0], run == mates[-1])
+
+        def bias_and_gate(run):
+            e, begin, end, bank, column = RUNS[run]
             nc.vector.scalar_tensor_tensor(
-                y[:, begin:end], banks[e][:, : end - begin], bias[:, e : e + 1], gates[:, begin:end], ADD, MULT
+                y[:, begin:end], banks[bank][:, column : column + end - begin], bias[:, e : e + 1],
+                gate_columns(begin, end), ADD, MULT,
             )
 
-        def bias_alone(e):
-            begin, end = max(STARTS[e], SPLIT), STARTS[e + 1]
+        def bias_alone(run):
+            e, begin, end, bank, column = RUNS[run]
             nc.scalar.activation(
-                y[:, begin:end], banks[e][:, begin - STARTS[e] : end - STARTS[e]], IDENTITY, bias=bias[:, e : e + 1]
+                y[:, begin:end], banks[bank][:, column : column + end - begin], IDENTITY, bias=bias[:, e : e + 1]
             )
+
+        def scatter(lo, hi):
+            nc.scalar.activation(windows[1][:].indirect(entries(lo, hi)), y[:, lo:hi], COPY)
 
         for chunk, end, share in CHUNKS[0]:
             for lo in range(chunk, end, BLOCK):
@@ -182,21 +220,38 @@ def tile_moe_rag_lin_bias_kernel(
             quantize(1, chunk, end)
 
         gather_scales(*AHEAD, AHEAD[1], f"raw1_{AHEAD[1]}")
-        for lo, hi in PIECES:
-            gather_scales(lo, hi, T, f"scales{lo}")
-            gather_words(lo, hi, T, f"words{lo}")
-            for g in range(2):
-                for e in reversed(range(E)):
-                    if lo < STARTS[e + 1] <= hi:
-                        multiply(e, g)
-        for e in range(SHARED, E):
-            bias_alone(e)
-        for lo, hi, experts in ON_SCALAR:
-            for e in experts:
-                bias_and_gate(e)
-        for lo, hi, experts in ON_SCALAR:
-            nc.scalar.activation(windows[1][:].indirect(entries(lo, hi)), y[:, lo:hi], COPY)
-        nc.vector.tensor_tensor(windows[0][:].indirect(entries(SPLIT, T)), y[:, SPLIT:], gates[:, SPLIT:], MULT)
+        for g in range(2):
+            products(g, "7a")
+        gather_scales(0, STARTS[3], T, "scales0")
+        gather_words(0, STARTS[3], T, "words0")
+        for g in range(2):
+            products(g, "0", "1", "2")
+        gather_scales(STARTS[3], STARTS[5], T, "scales3")
+        products(0, "3", "4")
+        for run in ("7a", "0", "1", "2"):
+            bias_and_gate(run)
+        scatter(*AHEAD)
+        scatter(0, STARTS[3])
+        gather_words(STARTS[3], STARTS[5], T, 768)
+        products(1, "3", "4")
+        gather_scales(STARTS[5], STARTS[7], T, 0)
+        products(0, "6", "5b", "5a")
+        for run in ("3", "4"):
+            bias_and_gate(run)
+        scatter(STARTS[3], STARTS[4])
+        gather_words(STARTS[5], STARTS[7], T, 4096)
+        products(1, "6", "5b", "5a")
+        gather_scales(AHEAD[1], T, T, 7168)
+        gather_words(AHEAD[1], T, T, 7424)
+        for g in range(2):
+            products(g, "7b")
+        for run in ("6", "5b"):
+            bias_alone(run)
+        for run in ("5a", "7b"):
+            bias_and_gate(run)
+        scatter(STARTS[4], OWN[0])
+        scatter(AHEAD[1], T)
+        nc.vector.tensor_tensor(windows[0][:].indirect(entries(*OWN)), y[:, OWN[0] : OWN[1]], gate_columns(*OWN), MULT)
         for lo, hi in zip(STORES, STORES[1:]):
             nc.vector.tensor_tensor(result[:, lo:hi], windows[0][:, lo:hi], windows[1][:, lo:hi], ADD)
             nc.sync.dma_start(out[:, lo:hi], result[:, lo:hi])

@@ -37,19 +37,19 @@ CHUNKS = (
 )
 LAST_CHUNK = 256
 AHEAD = (STARTS[E - 1], T - LAST_CHUNK)
-OWN = (1024, STARTS[7])
+OWN = (STARTS[5], STARTS[7])
 RUNS = {
     "0": (0, STARTS[0], STARTS[1], 0, 0),
     "1": (1, STARTS[1], STARTS[2], 1, 0),
     "2": (2, STARTS[2], STARTS[3], 2, 0),
     "3": (3, STARTS[3], STARTS[4], 3, 0),
     "4": (4, STARTS[4], STARTS[5], 3, COUNTS[3]),
-    "5a": (5, STARTS[5], OWN[0], 4, 0),
-    "5b": (5, OWN[0], STARTS[6], 5, 0),
-    "6": (6, STARTS[6], STARTS[7], 5, STARTS[6] - OWN[0]),
+    "5": (5, STARTS[5], STARTS[6], 4, 0),
+    "6": (6, STARTS[6], STARTS[7], 5, 0),
     "7a": (7, STARTS[7], AHEAD[1], 6, 0),
     "7b": (7, AHEAD[1], T, 7, 0),
 }
+HELD = 1536 - 256
 STORES = (0, 256, 640, 1152, 1664, T)
 
 
@@ -119,13 +119,12 @@ def tile_moe_rag_lin_bias_kernel(
             return gates[base][:, lo - base : hi - base]
 
         load_words(7, E)
-        load_words(0, 5)
+        load_words(0, 3)
         nc.sync.dma_start(bias[:], b)
-        load_gates(*AHEAD, offset=0)
+        load_gates(*AHEAD, offset=HELD)
         load_gates(0, STARTS[3])
-        load_gates(STARTS[3], STARTS[4], offset=6912)
-        load_words(5, 7)
-        load_gates(STARTS[4], STARTS[7])
+        load_words(3, 7)
+        load_gates(STARTS[3], STARTS[7])
         load_gates(AHEAD[1], T)
 
         def rounding_views(g, chunk, lo, hi):
@@ -157,12 +156,12 @@ def tile_moe_rag_lin_bias_kernel(
             return turns.tile([P, hi - lo], dtype, name=name, offset=place, align_bytes=ALIGN)
 
         def gather_words(lo, hi, tokens, place):
-            second_words[lo] = gathered(lo, hi, U32, f"second_words{lo}", place)
-            nc.vector.tensor_copy(second_words[lo][:], token_words[1][:, :tokens].indirect(entries(lo, hi)))
+            second_words[lo] = gathered(lo, hi, U32, f"second_words{lo}", place)[:]
+            nc.vector.tensor_copy(second_words[lo], token_words[1][:, :tokens].indirect(entries(lo, hi)))
 
         def gather_scales(lo, hi, tokens, place):
-            slot_scales[lo] = gathered(lo, hi, U8, f"slot_scales{lo}", place)
-            nc.vector.tensor_copy(slot_scales[lo][:], token_scales[:, :tokens].indirect(entries(lo, hi)))
+            slot_scales[lo] = gathered(lo, hi, U8, f"slot_scales{lo}", place)[:]
+            nc.vector.tensor_copy(slot_scales[lo], token_scales[:, :tokens].indirect(entries(lo, hi)))
 
         def multiply(run, g, opens, closes):
             e, begin, end, bank, column = RUNS[run]
@@ -232,24 +231,30 @@ def tile_moe_rag_lin_bias_kernel(
             bias_and_gate(run)
         scatter(*AHEAD)
         scatter(0, STARTS[3])
-        gather_words(STARTS[3], STARTS[5], T, 768)
+        late_words = turns.tile([P, STARTS[7] - STARTS[3] + T - AHEAD[1]], U32, name="late_words", offset=HELD + 256, align_bytes=ALIGN)
+        late_scales = turns.tile([P, 1536], U8, name="late_scales", offset=0, align_bytes=ALIGN)
+
+        def late_gather(table, tile, window, lo, hi, column):
+            table[lo] = tile[:, column : column + hi - lo]
+            nc.vector.tensor_copy(table[lo], window[:].indirect(entries(lo, hi)))
+
+        late_gather(slot_scales, late_scales, token_scales, STARTS[5], STARTS[7], 0)
+        products(0, "6", "5")
+        late_gather(second_words, late_words, token_words[1], STARTS[6], STARTS[7], 768)
+        products(1, "6")
+        late_gather(second_words, late_words, token_words[1], STARTS[5], STARTS[6], 384)
+        products(1, "5")
+        late_gather(second_words, late_words, token_words[1], STARTS[3], STARTS[5], 0)
         products(1, "3", "4")
-        gather_scales(STARTS[5], STARTS[7], T, 0)
-        products(0, "6", "5b", "5a")
-        for run in ("3", "4"):
-            bias_and_gate(run)
-        scatter(STARTS[3], STARTS[4])
-        gather_words(STARTS[5], STARTS[7], T, 4096)
-        products(1, "6", "5b", "5a")
-        gather_scales(AHEAD[1], T, T, 7168)
-        gather_words(AHEAD[1], T, T, 7424)
+        late_gather(slot_scales, late_scales, token_scales, AHEAD[1], T, 768)
+        late_gather(second_words, late_words, token_words[1], AHEAD[1], T, 1152)
         for g in range(2):
             products(g, "7b")
-        for run in ("6", "5b"):
+        for run in ("6", "5"):
             bias_alone(run)
-        for run in ("5a", "7b"):
+        for run in ("3", "4", "7b"):
             bias_and_gate(run)
-        scatter(STARTS[4], OWN[0])
+        scatter(STARTS[3], STARTS[5])
         scatter(AHEAD[1], T)
         nc.vector.tensor_tensor(windows[0][:].indirect(entries(*OWN)), y[:, OWN[0] : OWN[1]], gate_columns(*OWN), MULT)
         for lo, hi in zip(STORES, STORES[1:]):

@@ -227,10 +227,13 @@ def tile_moe_rag_lin_bias_kernel(
             products(g, "0", "1", "2")
         gather_scales(STARTS[3], STARTS[5], T, "scales3")
         products(0, "3", "4")
-        for run in ("7a", "0", "1", "2"):
-            bias_and_gate(run)
+        bias_and_gate("7a")
+        for run in ("0", "1", "2"):
+            bias_alone(run)
+        sparse = keep.tile([P, STARTS[3]], F32, name="sparse", align_bytes=ALIGN)
+        nc.gpsimd.tensor_tensor(sparse[:], y[:, : STARTS[3]], gate_columns(0, STARTS[3]), MULT)
         scatter(*AHEAD)
-        scatter(0, STARTS[3])
+        nc.scalar.activation(windows[1][:].indirect(entries(0, STARTS[3])), sparse[:], COPY)
         late_words = turns.tile([P, STARTS[7] - STARTS[3] + T - AHEAD[1]], U32, name="late_words", offset=HELD + 256, align_bytes=ALIGN)
         late_scales = turns.tile([P, 1536], U8, name="late_scales", offset=0, align_bytes=ALIGN)
 

@@ -37,7 +37,10 @@ CHUNKS = (
 )
 LAST_CHUNK = 256
 AHEAD = (STARTS[E - 1], T - LAST_CHUNK)
+BEHIND = (AHEAD[1], T)
 OWN = (STARTS[5], STARTS[7])
+FIRST = (0, STARTS[3])
+MIDDLE = (STARTS[3], STARTS[5])
 RUNS = {
     "0": (0, STARTS[0], STARTS[1], 0, 0),
     "1": (1, STARTS[1], STARTS[2], 1, 0),
@@ -46,10 +49,9 @@ RUNS = {
     "4": (4, STARTS[4], STARTS[5], 3, COUNTS[3]),
     "5": (5, STARTS[5], STARTS[6], 4, 0),
     "6": (6, STARTS[6], STARTS[7], 5, 0),
-    "7a": (7, STARTS[7], AHEAD[1], 6, 0),
-    "7b": (7, AHEAD[1], T, 7, 0),
+    "ahead": (7, *AHEAD, 6, 0),
+    "behind": (7, *BEHIND, 7, 0),
 }
-HELD = 1536 - 256
 STORES = (0, 256, 640, 1152, 1664, T)
 
 
@@ -72,14 +74,14 @@ def tile_moe_rag_lin_bias_kernel(
         first_words = keep.tile([P, T], U32, name="first_words", align_bytes=ALIGN)
         rounded = [keep.tile([P, T * PACK], BF16, name=f"rounded{g}", align_bytes=ALIGN) for g in range(2)]
         y = keep.tile([P, T], F32, name="y", align_bytes=ALIGN)
-        windows = [keep.tile([P, (2 - w) * T], F32, name=f"window{w}", align_bytes=ALIGN) for w in range(2)]
+        windows = [keep.tile([P, T], F32, name=f"window{w}", align_bytes=ALIGN) for w in range(2)]
         result = keep.tile([P, T], F32, name="result", align_bytes=ALIGN)
         banks = [psum.tile([P, BANK], F32, name=f"bank{i}") for i in range(E)]
 
         nc.vector.memset(weight_scales[:].bitcast(I32), 0)
         nc.vector.memset(token_scales[:].bitcast(I32), 0)
         for window in windows:
-            nc.vector.memset(window[:, :T], 0.0)
+            nc.vector.memset(window[:], 0.0)
 
         raws = {}
         for g in range(2):
@@ -107,25 +109,29 @@ def tile_moe_rag_lin_bias_kernel(
 
         gates = {}
 
-        def load_gates(lo, hi, offset=None):
-            if offset is None:
-                gates[lo] = keep.tile([P, hi - lo], F32, name=f"gates{lo}", align_bytes=ALIGN)
-            else:
-                gates[lo] = turns.tile([P, hi - lo], F32, name=f"gates{lo}", offset=offset, align_bytes=ALIGN)
-            nc.sync.dma_start(gates[lo][:], gate[:, lo:hi])
+        def load_gates(tile, lo, hi):
+            gates[lo] = tile
+            nc.sync.dma_start(tile[:], gate[:, lo:hi])
+
+        def gate_tile(lo, hi):
+            return keep.tile([P, hi - lo], F32, name=f"gates{lo}", align_bytes=ALIGN)
 
         def gate_columns(lo, hi):
             base = max(first for first in gates if first <= lo)
             return gates[base][:, lo - base : hi - base]
 
+        late_slots = STARTS[7] - STARTS[3] + LAST_CHUNK
+        scales_end = OWN[1] - OWN[0] + LAST_CHUNK
+        first_gates = turns.tile([P, LAST_CHUNK], F32, name="first_gates", offset=scales_end - ALIGN, align_bytes=ALIGN)
+
         load_words(7, E)
         load_words(0, 3)
         nc.sync.dma_start(bias[:], b)
-        load_gates(*AHEAD, offset=HELD)
-        load_gates(0, STARTS[3])
+        load_gates(first_gates, *AHEAD)
+        load_gates(gate_tile(*FIRST), *FIRST)
         load_words(3, 7)
-        load_gates(STARTS[3], STARTS[7])
-        load_gates(AHEAD[1], T)
+        load_gates(gate_tile(MIDDLE[0], OWN[1]), MIDDLE[0], OWN[1])
+        load_gates(gate_tile(*BEHIND), *BEHIND)
 
         def rounding_views(g, chunk, lo, hi):
             dst = rounded[g][:, lo * PACK : hi * PACK].rearrange("p (c i t) -> p c t i", i=2, t=PACK)
@@ -150,18 +156,16 @@ def tile_moe_rag_lin_bias_kernel(
         second_words = {}
         slot_scales = {}
 
-        def gathered(lo, hi, dtype, name, place):
-            if isinstance(place, str):
-                return keep.tile([P, hi - lo], dtype, name=name, tag=place, align_bytes=ALIGN)
-            return turns.tile([P, hi - lo], dtype, name=name, offset=place, align_bytes=ALIGN)
+        def gather_words(target, lo, hi, tokens=T):
+            second_words[lo] = target
+            nc.vector.tensor_copy(target, token_words[1][:, :tokens].indirect(entries(lo, hi)))
 
-        def gather_words(lo, hi, tokens, place):
-            second_words[lo] = gathered(lo, hi, U32, f"second_words{lo}", place)[:]
-            nc.vector.tensor_copy(second_words[lo], token_words[1][:, :tokens].indirect(entries(lo, hi)))
+        def gather_scales(target, lo, hi, tokens=T):
+            slot_scales[lo] = target
+            nc.vector.tensor_copy(target, token_scales[:, :tokens].indirect(entries(lo, hi)))
 
-        def gather_scales(lo, hi, tokens, place):
-            slot_scales[lo] = gathered(lo, hi, U8, f"slot_scales{lo}", place)[:]
-            nc.vector.tensor_copy(slot_scales[lo], token_scales[:, :tokens].indirect(entries(lo, hi)))
+        def own_tile(dtype, lo, hi, tag):
+            return keep.tile([P, hi - lo], dtype, name=f"gathered_{tag}", tag=tag, align_bytes=ALIGN)[:]
 
         def multiply(run, g, opens, closes):
             e, begin, end, bank, column = RUNS[run]
@@ -187,24 +191,29 @@ def tile_moe_rag_lin_bias_kernel(
 
         def products(g, *runs):
             for run in runs:
-                mates = [r for r in runs if RUNS[r][3] == RUNS[run][3]]
+                mates = [other for other in runs if RUNS[other][3] == RUNS[run][3]]
                 multiply(run, g, run == mates[0], run == mates[-1])
 
-        def bias_and_gate(run):
+        def sums(run):
             e, begin, end, bank, column = RUNS[run]
-            nc.vector.scalar_tensor_tensor(
-                y[:, begin:end], banks[bank][:, column : column + end - begin], bias[:, e : e + 1],
-                gate_columns(begin, end), ADD, MULT,
-            )
+            return banks[bank][:, column : column + end - begin]
+
+        def bias_of(run):
+            e = RUNS[run][0]
+            return bias[:, e : e + 1]
+
+        def bias_and_gate(run, target):
+            e, begin, end, bank, column = RUNS[run]
+            nc.vector.scalar_tensor_tensor(target, sums(run), bias_of(run), gate_columns(begin, end), ADD, MULT)
+
+        def results(run):
+            return y[:, RUNS[run][1] : RUNS[run][2]]
 
         def bias_alone(run):
-            e, begin, end, bank, column = RUNS[run]
-            nc.scalar.activation(
-                y[:, begin:end], banks[bank][:, column : column + end - begin], IDENTITY, bias=bias[:, e : e + 1]
-            )
+            nc.scalar.activation(results(run), sums(run), IDENTITY, bias=bias_of(run))
 
-        def scatter(lo, hi):
-            nc.scalar.activation(windows[1][:].indirect(entries(lo, hi)), y[:, lo:hi], COPY)
+        def scatter(values, lo, hi):
+            nc.scalar.activation(windows[1][:].indirect(entries(lo, hi)), values, COPY)
 
         for chunk, end, share in CHUNKS[0]:
             for lo in range(chunk, end, BLOCK):
@@ -215,51 +224,52 @@ def tile_moe_rag_lin_bias_kernel(
         for chunk, end, share in CHUNKS[1]:
             round_block(1, chunk, chunk + share, chunk, end)
             if end == T:
-                gather_words(*AHEAD, AHEAD[1], "ahead_words")
+                gather_words(own_tile(U32, *AHEAD, "ahead_words"), *AHEAD, tokens=AHEAD[1])
             quantize(1, chunk, end)
 
-        gather_scales(*AHEAD, AHEAD[1], f"raw1_{AHEAD[1]}")
+        gather_scales(own_tile(U8, *AHEAD, f"raw1_{AHEAD[1]}"), *AHEAD, tokens=AHEAD[1])
         for g in range(2):
-            products(g, "7a")
-        gather_scales(0, STARTS[3], T, "scales0")
-        gather_words(0, STARTS[3], T, "words0")
+            products(g, "ahead")
+
+        gather_scales(own_tile(U8, *FIRST, "first_scales"), *FIRST)
+        gather_words(own_tile(U32, *FIRST, "first_experts_words"), *FIRST)
         for g in range(2):
             products(g, "0", "1", "2")
-        gather_scales(STARTS[3], STARTS[5], T, "scales3")
+        gather_scales(own_tile(U8, *MIDDLE, "middle_scales"), *MIDDLE)
         products(0, "3", "4")
-        bias_and_gate("7a")
-        for run in ("0", "1", "2"):
+
+        first_gated = keep.tile([P, FIRST[1]], F32, name="first_gated", align_bytes=ALIGN)
+        bias_and_gate("ahead", results("ahead"))
+        bias_and_gate("0", first_gated[:, : STARTS[1]])
+        for run in ("1", "2"):
             bias_alone(run)
-        sparse = keep.tile([P, STARTS[3]], F32, name="sparse", align_bytes=ALIGN)
-        nc.gpsimd.tensor_tensor(sparse[:], y[:, : STARTS[3]], gate_columns(0, STARTS[3]), MULT)
-        scatter(*AHEAD)
-        nc.scalar.activation(windows[1][:].indirect(entries(0, STARTS[3])), sparse[:], COPY)
-        late_words = turns.tile([P, STARTS[7] - STARTS[3] + T - AHEAD[1]], U32, name="late_words", offset=HELD + 256, align_bytes=ALIGN)
-        late_scales = turns.tile([P, 1536], U8, name="late_scales", offset=0, align_bytes=ALIGN)
+        nc.gpsimd.tensor_tensor(
+            first_gated[:, STARTS[1] :], y[:, STARTS[1] : STARTS[3]], gate_columns(STARTS[1], STARTS[3]), MULT
+        )
+        scatter(y[:, AHEAD[0] : AHEAD[1]], *AHEAD)
+        scatter(first_gated[:], *FIRST)
 
-        def late_gather(table, tile, window, lo, hi, column):
-            table[lo] = tile[:, column : column + hi - lo]
-            nc.vector.tensor_copy(table[lo], window[:].indirect(entries(lo, hi)))
-
-        late_gather(slot_scales, late_scales, token_scales, STARTS[5], STARTS[7], 0)
+        late_words = turns.tile([P, late_slots], U32, name="late_words", offset=scales_end, align_bytes=ALIGN)
+        late_scales = turns.tile([P, scales_end], U8, name="late_scales", offset=0, align_bytes=ALIGN)
+        gather_scales(late_scales[:, : OWN[1] - OWN[0]], *OWN)
         products(0, "6", "5")
-        late_gather(second_words, late_words, token_words[1], STARTS[6], STARTS[7], 768)
-        products(1, "6")
-        late_gather(second_words, late_words, token_words[1], STARTS[5], STARTS[6], 384)
-        products(1, "5")
-        late_gather(second_words, late_words, token_words[1], STARTS[3], STARTS[5], 0)
-        products(1, "3", "4")
-        late_gather(slot_scales, late_scales, token_scales, AHEAD[1], T, 768)
-        late_gather(second_words, late_words, token_words[1], AHEAD[1], T, 1152)
+        for lo, hi, runs in ((STARTS[6], STARTS[7], ("6",)), (STARTS[5], STARTS[6], ("5",)), (*MIDDLE, ("3", "4"))):
+            gather_words(late_words[:, lo - MIDDLE[0] : hi - MIDDLE[0]], lo, hi)
+            products(1, *runs)
+        gather_scales(late_scales[:, OWN[1] - OWN[0] :], *BEHIND)
+        gather_words(late_words[:, late_slots - LAST_CHUNK :], *BEHIND)
         for g in range(2):
-            products(g, "7b")
+            products(g, "behind")
+
         for run in ("6", "5"):
             bias_alone(run)
-        for run in ("3", "4", "7b"):
-            bias_and_gate(run)
-        scatter(STARTS[3], STARTS[5])
-        scatter(AHEAD[1], T)
-        nc.vector.tensor_tensor(windows[0][:].indirect(entries(*OWN)), y[:, OWN[0] : OWN[1]], gate_columns(*OWN), MULT)
+        for run in ("3", "4", "behind"):
+            bias_and_gate(run, results(run))
+        for lo, hi in (MIDDLE, BEHIND):
+            scatter(y[:, lo:hi], lo, hi)
+        nc.vector.tensor_tensor(
+            windows[0][:].indirect(entries(*OWN)), y[:, OWN[0] : OWN[1]], gate_columns(*OWN), MULT
+        )
         for lo, hi in zip(STORES, STORES[1:]):
             nc.vector.tensor_tensor(result[:, lo:hi], windows[0][:, lo:hi], windows[1][:, lo:hi], ADD)
             nc.sync.dma_start(out[:, lo:hi], result[:, lo:hi])

@@ -89,8 +89,8 @@ def tile_moe_rag_lin_bias_kernel(
             for lo, hi, share in CHUNKS[g]:
                 raws[g, lo] = keep.tile([P, PACK, hi - lo], F32, name=f"raw{g}_{lo}", tag=f"raw{g}_{lo}", align_bytes=ALIGN)
                 nc.sync.dma_start(raws[g, lo][:], rows[:, :, lo:hi])
-                if (g, lo) == (0, 0):
-                    nc.sync.dma_start(offsets[:], offs)
+            if g == 0:
+                nc.sync.dma_start(offsets[:], offs)
 
         words8 = w8_words.rearrange("e a p n r -> p (e a) (n r)")
         words4 = w4_words.rearrange("e a p n -> p (e a) n")

@@ -50,9 +50,9 @@ RUNS = {
     "5": (5, STARTS[5], STARTS[6], 4, 0),
     "6": (6, STARTS[6], STARTS[7], 5, 0),
     "ahead": (7, *AHEAD, 6, 0),
-    "behind": (7, *BEHIND, 7, 0),
+    "behind": (7, *BEHIND, 2, 0),
 }
-STORES = (0, 256, 640, 1152, 1664, T)
+STORES = (0, 384, 768, 1216, 1664, T)
 
 
 def tile_moe_rag_lin_bias_kernel(
@@ -61,12 +61,9 @@ def tile_moe_rag_lin_bias_kernel(
     nc = tc.nc
     with ExitStack() as ctx:
         keep = ctx.enter_context(tc.tile_pool(name="keep", bufs=1))
-        turns = ctx.enter_context(tc.tile_pool(name="turns", bufs=1))
         psum = ctx.enter_context(tc.psum_pool(name="psum", bufs=1))
 
         offsets = keep.tile([P, T // GROUP], U16, name="offsets")
-        w8 = keep.tile([P, E * N * 4], U8, name="w8", align_bytes=ALIGN)
-        w4 = keep.tile([P, E * N * 2], U8, name="w4", align_bytes=ALIGN)
         weight_scales = keep.tile([P, E * N], U8, name="weight_scales", align_bytes=ALIGN)
         bias = keep.tile([P, E], F32, name="bias")
         token_scales = keep.tile([P, T], U8, name="token_scales", align_bytes=ALIGN)
@@ -76,7 +73,7 @@ def tile_moe_rag_lin_bias_kernel(
         y = keep.tile([P, T], F32, name="y", align_bytes=ALIGN)
         windows = [keep.tile([P, T], F32, name=f"window{w}", align_bytes=ALIGN) for w in range(2)]
         result = keep.tile([P, T], F32, name="result", align_bytes=ALIGN)
-        banks = [psum.tile([P, BANK], F32, name=f"bank{i}") for i in range(E)]
+        banks = [psum.tile([P, BANK], F32, name=f"bank{i}") for i in range(E - 1)]
 
         nc.vector.memset(weight_scales[:].bitcast(I32), 0)
         nc.vector.memset(token_scales[:].bitcast(I32), 0)
@@ -95,10 +92,14 @@ def tile_moe_rag_lin_bias_kernel(
         words8 = w8_words.rearrange("e a p n r -> p (e a) (n r)")
         words4 = w4_words.rearrange("e a p n -> p (e a) n")
 
+        weights = {}
+
         def load_words(lo, hi):
-            for tile, words in ((w4, words4), (w8, words8)):
-                view = tile[:].bitcast(I32).rearrange("p (e n) -> p e n", e=E)
-                nc.sync.dma_start(view[:, lo:hi], words.bitcast(I32)[:, lo:hi])
+            for g, words, width in ((1, words4, 2 * N), (0, words8, 4 * N)):
+                tile = keep.tile([P, (hi - lo) * width], U8, name=f"weights{g}_{lo}", tag=f"weights{g}_{lo}", align_bytes=ALIGN)
+                nc.sync.dma_start(tile[:].bitcast(I32).rearrange("p (e n) -> p e n", e=hi - lo), words.bitcast(I32)[:, lo:hi])
+                for e in range(lo, hi):
+                    weights[g, e] = tile[:, (e - lo) * width : (e - lo + 1) * width]
 
         planes = weight_scales[:].bitcast(I32).rearrange("p (e n) -> p e n", e=E)
         for quadrant in range(P // QUADRANT):
@@ -109,29 +110,22 @@ def tile_moe_rag_lin_bias_kernel(
 
         gates = {}
 
-        def load_gates(tile, lo, hi):
-            gates[lo] = tile
-            nc.sync.dma_start(tile[:], gate[:, lo:hi])
-
-        def gate_tile(lo, hi):
-            return keep.tile([P, hi - lo], F32, name=f"gates{lo}", align_bytes=ALIGN)
+        def load_gates(lo, hi):
+            gates[lo] = keep.tile([P, hi - lo], F32, name=f"gates{lo}", align_bytes=ALIGN)
+            nc.sync.dma_start(gates[lo][:], gate[:, lo:hi])
 
         def gate_columns(lo, hi):
             base = max(first for first in gates if first <= lo)
             return gates[base][:, lo - base : hi - base]
 
-        late_slots = STARTS[7] - STARTS[3] + LAST_CHUNK
-        scales_end = OWN[1] - OWN[0] + LAST_CHUNK
-        first_gates = turns.tile([P, LAST_CHUNK], F32, name="first_gates", offset=scales_end - ALIGN, align_bytes=ALIGN)
-
         load_words(7, E)
         load_words(0, 3)
         nc.sync.dma_start(bias[:], b)
-        load_gates(first_gates, *AHEAD)
-        load_gates(gate_tile(*FIRST), *FIRST)
+        load_gates(*AHEAD)
+        load_gates(*FIRST)
         load_words(3, 7)
-        load_gates(gate_tile(MIDDLE[0], OWN[1]), MIDDLE[0], OWN[1])
-        load_gates(gate_tile(*BEHIND), *BEHIND)
+        load_gates(*BEHIND)
+        load_gates(MIDDLE[0], OWN[1])
 
         def rounding_views(g, chunk, lo, hi):
             dst = rounded[g][:, lo * PACK : hi * PACK].rearrange("p (c i t) -> p c t i", i=2, t=PACK)
@@ -177,14 +171,14 @@ def tile_moe_rag_lin_bias_kernel(
                 acc = banks[bank][:, column + c0 - begin : column + c1 - begin]
                 if g == 0:
                     nc.tensor.matmul_mx(
-                        out=acc, lhsT=w8[:, e * N * 4 : (e + 1) * N * 4].bitcast(FP8X4), lhsT_scale=weight_scales[E4M3_ROW:, columns],
+                        out=acc, lhsT=weights[0, e].bitcast(FP8X4), lhsT_scale=weight_scales[E4M3_ROW:, columns],
                         rhs=first_words[:, c0:c1].bitcast(FP8X4), rhs_scale=scales[E4M3_ROW:, c0 - base : c1 - base],
                         start=opens and c0 == begin, stop=False,
                     )
                 else:
                     first = max(lo for lo in second_words if lo <= c0)
                     nc.tensor.matmul_mx(
-                        out=acc, lhsT=w4[:, e * N * 2 : (e + 1) * N * 2].bitcast(FP4X4), lhsT_scale=weight_scales[:, columns],
+                        out=acc, lhsT=weights[1, e].bitcast(FP4X4), lhsT_scale=weight_scales[:, columns],
                         rhs=second_words[first][:, c0 - first : c1 - first].bitcast(FP8X4), rhs_scale=scales[:, c0 - base : c1 - base],
                         start=False, stop=closes and c1 == end,
                     )
@@ -235,37 +229,35 @@ def tile_moe_rag_lin_bias_kernel(
         gather_words(own_tile(U32, *FIRST, "first_experts_words"), *FIRST)
         for g in range(2):
             products(g, "0", "1", "2")
-        gather_scales(own_tile(U8, *MIDDLE, "middle_scales"), *MIDDLE)
-        products(0, "3", "4")
+        for lo, hi in (BEHIND, (STARTS[6], STARTS[7])):
+            gather_words(own_tile(U32, lo, hi, f"words{lo}"), lo, hi)
 
-        first_gated = keep.tile([P, FIRST[1]], F32, name="first_gated", align_bytes=ALIGN)
-        bias_and_gate("ahead", results("ahead"))
-        bias_and_gate("0", first_gated[:, : STARTS[1]])
-        for run in ("1", "2"):
-            bias_alone(run)
-        nc.gpsimd.tensor_tensor(
-            first_gated[:, STARTS[1] :], y[:, STARTS[1] : STARTS[3]], gate_columns(STARTS[1], STARTS[3]), MULT
-        )
-        scatter(y[:, AHEAD[0] : AHEAD[1]], *AHEAD)
-        scatter(first_gated[:], *FIRST)
+        gated = keep.tile([P, FIRST[1] + LAST_CHUNK], F32, name="gated", align_bytes=ALIGN)
+        for runs, (lo, hi), target in ((("ahead",), AHEAD, gated[:, FIRST[1] :]), (("0", "1", "2"), FIRST, gated[:, : FIRST[1]])):
+            for run in runs:
+                bias_alone(run)
+            nc.gpsimd.tensor_tensor(target, y[:, lo:hi], gate_columns(lo, hi), MULT)
+        scatter(gated[:, FIRST[1] :], *AHEAD)
+        scatter(gated[:, : FIRST[1]], *FIRST)
 
-        late_words = turns.tile([P, late_slots], U32, name="late_words", offset=scales_end, align_bytes=ALIGN)
-        late_scales = turns.tile([P, scales_end], U8, name="late_scales", offset=0, align_bytes=ALIGN)
-        gather_scales(late_scales[:, : OWN[1] - OWN[0]], *OWN)
-        products(0, "6", "5")
-        for lo, hi, runs in ((STARTS[6], STARTS[7], ("6",)), (STARTS[5], STARTS[6], ("5",)), (*MIDDLE, ("3", "4"))):
-            gather_words(late_words[:, lo - MIDDLE[0] : hi - MIDDLE[0]], lo, hi)
-            products(1, *runs)
-        gather_scales(late_scales[:, OWN[1] - OWN[0] :], *BEHIND)
-        gather_words(late_words[:, late_slots - LAST_CHUNK :], *BEHIND)
+        gather_scales(own_tile(U8, *BEHIND, "behind_scales"), *BEHIND)
         for g in range(2):
             products(g, "behind")
+        gather_scales(own_tile(U8, *OWN, "own_scales"), *OWN)
+        for g in range(2):
+            products(g, "6")
+        products(0, "5")
+        gather_scales(own_tile(U8, *MIDDLE, "middle_scales"), *MIDDLE)
+        products(0, "3", "4")
+        for lo, hi, runs in ((STARTS[5], STARTS[6], ("5",)), (*MIDDLE, ("3", "4"))):
+            gather_words(own_tile(U32, lo, hi, f"words{lo}"), lo, hi)
+            products(1, *runs)
 
-        for run in ("6", "5"):
-            bias_alone(run)
-        for run in ("3", "4", "behind"):
+        bias_alone("6")
+        nc.vector.tensor_scalar_add(results("5"), sums("5"), bias_of("5"))
+        for run in ("behind", "3", "4"):
             bias_and_gate(run, results(run))
-        for lo, hi in (MIDDLE, BEHIND):
+        for lo, hi in (BEHIND, MIDDLE):
             scatter(y[:, lo:hi], lo, hi)
         nc.vector.tensor_tensor(
             windows[0][:].indirect(entries(*OWN)), y[:, OWN[0] : OWN[1]], gate_columns(*OWN), MULT

from contextlib import ExitStack

import concourse.mybir as mybir

K, T, E, N = 1024, 2048, 8, 128
COUNTS = (128, 128, 128, 256, 128, 384, 384, 512)
STARTS = tuple(sum(COUNTS[:e]) for e in range(E + 1))
FLOPS = 2 * T * K * N

P = 128
PACK = 4
K_PASS = P * PACK
BANK = 512
GROUP = 16
QUADRANT = 32
ALIGN = 256
E4M3_ROW = 4
BLOCK = 512
WIDE = 256

F32 = mybir.dt.float32
BF16 = mybir.dt.bfloat16
I32 = mybir.dt.int32
U32 = mybir.dt.uint32
U16 = mybir.dt.uint16
U8 = mybir.dt.uint8
FP8X4 = mybir.dt.float8_e4m3fn_x4
FP4X4 = mybir.dt.float4_e2m1fn_x4
COPY = mybir.ActivationFunctionType.Copy
IDENTITY = mybir.ActivationFunctionType.Identity
ADD = mybir.AluOpType.add
MULT = mybir.AluOpType.mult

CHUNKS = (
    ((0, 1280, 640), (1280, 2048, 384)),
    ((0, 512, 0), (512, 1024, 0), (1024, 1536, 192), (1536, 1792, 96), (1792, 2048, 96)),
)
LAST_CHUNK = 256
AHEAD = (STARTS[E - 1], T - LAST_CHUNK)
BEHIND = (AHEAD[1], T)
OWN = (STARTS[5], STARTS[7])
FIRST = (0, STARTS[3])
MIDDLE = (STARTS[3], STARTS[5])
RUNS = {
    "0": (0, STARTS[0], STARTS[1], 0, 0),
    "1": (1, STARTS[1], STARTS[2], 1, 0),
    "2": (2, STARTS[2], STARTS[3], 2, 0),
    "3": (3, STARTS[3], STARTS[4], 3, 0),
    "4": (4, STARTS[4], STARTS[5], 3, COUNTS[3]),
    "5": (5, STARTS[5], STARTS[6], 4, 0),
    "6": (6, STARTS[6], STARTS[7], 5, 0),
    "ahead": (7, *AHEAD, 6, 0),
    "behind": (7, *BEHIND, 2, 0),
}
STORES = (0, 384, 768, 1216, 1664, T)


def tile_moe_rag_lin_bias_kernel(
    tc, xT, w8_words, w8_scales, w4_words, w4_scales, b, gate, offs, out
):
    nc = tc.nc
    with ExitStack() as ctx:
        keep = ctx.enter_context(tc.tile_pool(name="keep", bufs=1))
        psum = ctx.enter_context(tc.psum_pool(name="psum", bufs=1))

        offsets = keep.tile([P, T // GROUP], U16, name="offsets")
        weight_scales = keep.tile([P, E * N], U8, name="weight_scales", align_bytes=ALIGN)
        bias = keep.tile([P, E], F32, name="bias")
        token_scales = keep.tile([P, T], U8, name="token_scales", align_bytes=ALIGN)
        token_words = [keep.tile([P, (2 - g) * T], U32, name=f"token_words{g}", align_bytes=ALIGN) for g in range(2)]
        first_words = keep.tile([P, T], U32, name="first_words", align_bytes=ALIGN)
        rounded = [keep.tile([P, T * PACK], BF16, name=f"rounded{g}", align_bytes=ALIGN) for g in range(2)]
        y = keep.tile([P, T], F32, name="y", align_bytes=ALIGN)
        windows = [keep.tile([P, T], F32, name=f"window{w}", align_bytes=ALIGN) for w in range(2)]
        result = keep.tile([P, T], F32, name="result", align_bytes=ALIGN)
        banks = [psum.tile([P, BANK], F32, name=f"bank{i}") for i in range(E - 1)]

        nc.vector.memset(weight_scales[:].bitcast(I32), 0)
        nc.vector.memset(token_scales[:].bitcast(I32), 0)
        for window in windows:
            nc.vector.memset(window[:], 0.0)

        raws = {}
        for g in range(2):
            rows = xT[K_PASS * g : K_PASS * (g + 1), :].rearrange("(p j) w -> p j w", j=PACK)
            for lo, hi, share in CHUNKS[g]:
                raws[g, lo] = keep.tile([P, PACK, hi - lo], F32, name=f"raw{g}_{lo}", tag=f"raw{g}_{lo}", align_bytes=ALIGN)
                nc.sync.dma_start(raws[g, lo][:], rows[:, :, lo:hi])
            if g == 0:
                nc.sync.dma_start(offsets[:], offs)

        words8 = w8_words.rearrange("e a p n r -> p (e a) (n r)")
        words4 = w4_words.rearrange("e a p n -> p (e a) n")

        weights = {}

        def load_words(lo, hi):
            for g, words, width in ((1, words4, 2 * N), (0, words8, 4 * N)):
                tile = keep.tile([P, (hi - lo) * width], U8, name=f"weights{g}_{lo}", tag=f"weights{g}_{lo}", align_bytes=ALIGN)
                nc.sync.dma_start(tile[:].bitcast(I32).rearrange("p (e n) -> p e n", e=hi - lo), words.bitcast(I32)[:, lo:hi])
                for e in range(lo, hi):
                    weights[g, e] = tile[:, (e - lo) * width : (e - lo + 1) * width]

        planes = weight_scales[:].bitcast(I32).rearrange("p (e n) -> p e n", e=E)
        for quadrant in range(P // QUADRANT):
            for scales, first_row in ((w8_scales, E4M3_ROW), (w4_scales, 0)):
                start = QUADRANT * quadrant + first_row
                source = scales[:, 0, 4 * quadrant : 4 * quadrant + 4, :].rearrange("e q n -> q e n")
                nc.sync.dma_start(planes[start : start + 4], source.bitcast(I32))

        gates = {}

        def load_gates(lo, hi):
            gates[lo] = keep.tile([P, hi - lo], F32, name=f"gates{lo}", align_bytes=ALIGN)
            nc.sync.dma_start(gates[lo][:], gate[:, lo:hi])

        def gate_columns(lo, hi):
            base = max(first for first in gates if first <= lo)
            return gates[base][:, lo - base : hi - base]

        load_words(7, E)
        load_words(0, 3)
        nc.sync.dma_start(bias[:], b)
        load_gates(*AHEAD)
        load_gates(*FIRST)
        load_words(3, 7)
        load_gates(*BEHIND)
        load_gates(MIDDLE[0], OWN[1])

        def rounding_views(g, chunk, lo, hi):
            dst = rounded[g][:, lo * PACK : hi * PACK].rearrange("p (c i t) -> p c t i", i=2, t=PACK)
            return dst, raws[g, chunk][:, :, lo - chunk : hi - chunk].rearrange("p t (c i) -> p c t i", i=2)

        def round_block(g, chunk, border, lo, hi):
            if lo < border:
                nc.vector.tensor_copy(*rounding_views(g, chunk, lo, min(hi, border)))
            if border < hi:
                nc.scalar.activation(*rounding_views(g, chunk, max(lo, border), hi), COPY)

        def quantize(g, lo, hi):
            nc.vector.quantize_mx(
                out=token_words[g][:, lo:hi].bitcast(FP8X4),
                scales=token_scales[E4M3_ROW:, lo:hi] if g == 0 else token_scales[:, lo:hi],
                in_=rounded[g][:, lo * PACK : hi * PACK],
            )

        def entries(lo, hi):
            return offsets[:, lo // GROUP : hi // GROUP]

        second_words = {}
        slot_scales = {}

        def gather_words(target, lo, hi, tokens=T):
            second_words[lo] = target
            nc.vector.tensor_copy(target, token_words[1][:, :tokens].indirect(entries(lo, hi)))

        def gather_scales(target, lo, hi, tokens=T):
            slot_scales[lo] = target
            nc.vector.tensor_copy(target, token_scales[:, :tokens].indirect(entries(lo, hi)))

        def own_tile(dtype, lo, hi, tag):
            return keep.tile([P, hi - lo], dtype, name=f"gathered_{tag}", tag=tag, align_bytes=ALIGN)[:]

        def multiply(run, g, opens, closes):
            e, begin, end, bank, column = RUNS[run]
            columns = slice(e * N, (e + 1) * N)
            for c0 in range(begin, end, WIDE):
                c1 = min(c0 + WIDE, end)
                base = max(lo for lo in slot_scales if lo <= c0)
                scales = slot_scales[base]
                acc = banks[bank][:, column + c0 - begin : column + c1 - begin]
                if g == 0:
                    nc.tensor.matmul_mx(
                        out=acc, lhsT=weights[0, e].bitcast(FP8X4), lhsT_scale=weight_scales[E4M3_ROW:, columns],
                        rhs=first_words[:, c0:c1].bitcast(FP8X4), rhs_scale=scales[E4M3_ROW:, c0 - base : c1 - base],
                        start=opens and c0 == begin, stop=False,
                    )
                else:
                    first = max(lo for lo in second_words if lo <= c0)
                    nc.tensor.matmul_mx(
                        out=acc, lhsT=weights[1, e].bitcast(FP4X4), lhsT_scale=weight_scales[:, columns],
                        rhs=second_words[first][:, c0 - first : c1 - first].bitcast(FP8X4), rhs_scale=scales[:, c0 - base : c1 - base],
                        start=False, stop=closes and c1 == end,
                    )

        def products(g, *runs):
            for run in runs:
                mates = [other for other in runs if RUNS[other][3] == RUNS[run][3]]
                multiply(run, g, run == mates[0], run == mates[-1])

        def sums(run):
            e, begin, end, bank, column = RUNS[run]
            return banks[bank][:, column : column + end - begin]

        def bias_of(run):
            e = RUNS[run][0]
            return bias[:, e : e + 1]

        def bias_and_gate(run, target):
            e, begin, end, bank, column = RUNS[run]
            nc.vector.scalar_tensor_tensor(target, sums(run), bias_of(run), gate_columns(begin, end), ADD, MULT)

        def results(run):
            return y[:, RUNS[run][1] : RUNS[run][2]]

        def bias_alone(run):
            nc.scalar.activation(results(run), sums(run), IDENTITY, bias=bias_of(run))

        def scatter(values, lo, hi):
            nc.scalar.activation(windows[1][:].indirect(entries(lo, hi)), values, COPY)

        for chunk, end, share in CHUNKS[0]:
            for lo in range(chunk, end, BLOCK):
                round_block(0, chunk, chunk + share, lo, min(lo + BLOCK, end))
                quantize(0, lo, min(lo + BLOCK, end))
        nc.vector.tensor_copy(first_words[:], token_words[0][:].indirect(offsets[:]))

        for chunk, end, share in CHUNKS[1]:
            round_block(1, chunk, chunk + share, chunk, end)
            if end == T:
                gather_words(own_tile(U32, *AHEAD, "ahead_words"), *AHEAD, tokens=AHEAD[1])
            quantize(1, chunk, end)

        gather_scales(own_tile(U8, *AHEAD, f"raw1_{AHEAD[1]}"), *AHEAD, tokens=AHEAD[1])
        for g in range(2):
            products(g, "ahead")

        gather_scales(own_tile(U8, *FIRST, "first_scales"), *FIRST)
        gather_words(own_tile(U32, *FIRST, "first_experts_words"), *FIRST)
        for g in range(2):
            products(g, "0", "1", "2")
        for lo, hi in (BEHIND, (STARTS[6], STARTS[7])):
            gather_words(own_tile(U32, lo, hi, f"words{lo}"), lo, hi)

        gated = keep.tile([P, FIRST[1] + LAST_CHUNK], F32, name="gated", align_bytes=ALIGN)
        for runs, (lo, hi), target in ((("ahead",), AHEAD, gated[:, FIRST[1] :]), (("0", "1", "2"), FIRST, gated[:, : FIRST[1]])):
            for run in runs:
                bias_alone(run)
            nc.gpsimd.tensor_tensor(target, y[:, lo:hi], gate_columns(lo, hi), MULT)
        scatter(gated[:, FIRST[1] :], *AHEAD)
        scatter(gated[:, : FIRST[1]], *FIRST)

        gather_scales(own_tile(U8, *BEHIND, "behind_scales"), *BEHIND)
        for g in range(2):
            products(g, "behind")
        gather_scales(own_tile(U8, *OWN, "own_scales"), *OWN)
        for g in range(2):
            products(g, "6")
        products(0, "5")
        gather_scales(own_tile(U8, *MIDDLE, "middle_scales"), *MIDDLE)
        products(0, "3", "4")
        for lo, hi, runs in ((STARTS[5], STARTS[6], ("5",)), (*MIDDLE, ("3", "4"))):
            gather_words(own_tile(U32, lo, hi, f"words{lo}"), lo, hi)
            products(1, *runs)

        bias_alone("6")
        nc.vector.tensor_scalar_add(results("5"), sums("5"), bias_of("5"))
        for run in ("behind", "3", "4"):
            bias_and_gate(run, results(run))
        for lo, hi in (BEHIND, MIDDLE):
            scatter(y[:, lo:hi], lo, hi)
        nc.vector.tensor_tensor(
            windows[0][:].indirect(entries(*OWN)), y[:, OWN[0] : OWN[1]], gate_columns(*OWN), MULT
        )
        for lo, hi in zip(STORES, STORES[1:]):
            nc.vector.tensor_tensor(result[:, lo:hi], windows[0][:, lo:hi], windows[1][:, lo:hi], ADD)
            nc.sync.dma_start(out[:, lo:hi], result[:, lo:hi])
